import numpy as np, ml_dtypes
CORES = [2,3,42,43,82,83,122,123]
N = 8
import mx_ref
BF = ml_dtypes.bfloat16
def entries(a):
    return np.ascontiguousarray(a.T).reshape(-1)
def table(e):
    return np.ascontiguousarray(np.reshape(e, (-1, 16)).T).astype(np.int32)
def tile(rs):
    return np.stack(rs, axis=2).reshape(128, -1).astype(BF)
def cut(t, i, w=512):
    return t[:, w * i:w * i + w]
def f(rng, *shape):
    return mx_ref.flush((rng.standard_normal(shape, dtype=np.float32) * np.exp2(rng.integers(-2, 3, shape[:-1] + (1,)))).astype(BF))
def wide(rng, *shape, cols=0):
    v = rng.standard_normal(shape, dtype=np.float32) * np.exp2(rng.integers(-12, 13, shape)).astype(np.float32)
    if cols: v *= np.repeat(np.exp2(rng.integers(-cols, cols + 1, shape[:-2] + (1, shape[-1] // 4))) * (rng.random(shape[:-2] + (1, shape[-1] // 4)) > 0.0625), 4, axis=-1).astype(np.float32)
    return mx_ref.flush(v.astype(BF))
T, TG, C1, C2 = 512, 256, 320, 64
def layer(rng, C, M, own=0.25, full=False, hub=False, neg=None):
    snd = np.full((N, N, C), -1); src = np.zeros((N, M, 4), int)
    for s in range(N):
        for r in range(N):
            if s != r and own < 1:
                n = C if full else rng.integers(1, C + 1)
                snd[s, r, rng.permutation(C)[:n]] = rng.choice(T, n, replace=False)
    h, k, c = rng.integers(0, N), rng.integers(0, T), rng.integers(0, C, N)
    if hub:
        for r in range(N):
            if r != h: snd[h, r, c[r]] = k
    for r in range(N):
        src[r] = rng.integers(0, T, (M, 4))
        if own < 1:
            far = T + np.flatnonzero(snd[:, r].reshape(-1) >= 0)
            src[r] = np.where(rng.random((M, 4)) < own, src[r], rng.choice(far, (M, 4)))
        if hub:
            e = k if r == h else T + h * C + c[r]
            src[r][:, 0] = e; src[r][rng.permutation(M)[:M // 4]] = e
            src[r] = rng.permuted(src[r], axis=1)
        if neg is not None:
            bad = np.flatnonzero(np.concatenate([neg[r]] + [(snd[s, r] >= 0) & neg[s][snd[s, r]] for s in range(N)]))
            src[r][rng.permutation(M)[:M // 2]] = rng.choice(bad, (M // 2, 4))
    return np.stack([table(a) for a in snd]), np.stack([table(a) for a in src])
def lists(rng, neg=None, **o):
    a, b = layer(rng, C1, T, neg=neg, **o); c, e = layer(rng, C2, TG, **o)
    return {"snd1": a, "src1": b, "snd2": c, "src2": e}
def setup_inputs(rng):
    return {"x": f(rng, N, 128, 4 * T), "w1": np.repeat(f(rng, 1, 128, 4 * 512), N, axis=0), "w2": np.repeat(f(rng, 1, 128, 512), N, axis=0), **lists(rng)}
def setup_inputs_foreign(rng):
    return {**setup_inputs(rng), **lists(rng, own=0, full=True)}
def setup_inputs_hub(rng):
    return {**setup_inputs(rng), **lists(rng, hub=True)}
def setup_inputs_negative(rng):
    d = setup_inputs(rng)
    neg = np.stack([rng.permutation(T) < T // 2 for r in range(N)])
    v = np.abs(d["x"]).reshape(N, 128, T, 4)
    d["x"] = np.where(neg[:, None, :, None], -v, v).reshape(N, 128, 4 * T)
    d["w1"] = np.abs(d["w1"])
    return {**d, **lists(rng, neg=neg)}
def setup_inputs_self(rng):
    return {**setup_inputs(rng), **lists(rng, own=1)}
def setup_inputs_spread(rng):
    d = setup_inputs(rng); d["x"] = wide(rng, N, 128, 4 * T); return d
def check_inputs(d):
    b = []
    for k in ("w1", "w2"):
        if any(d[k][r].tobytes() != d[k][0].tobytes() for r in range(N)): b.append(k)
    for l, C in (("1", C1), ("2", C2)):
        snd = np.stack([entries(a) for a in d["snd" + l]]).reshape(N, N, C)
        if snd.min() < -1 or snd.max() >= T: b.append("snd" + l)
        for r in range(N):
            if (snd[r, r] != -1).any(): b.append("snd" + l)
            ok = np.concatenate([np.ones(T, bool), snd[:, r].reshape(-1) >= 0])
            e = entries(d["src" + l][r])
            if e.min() < 0 or e.max() >= T + N * C or not ok[e].all(): b.append("src" + l)
    return b
def most(v, snd, src, r, C):
    a = np.concatenate([v[r]] + [v[s][:, entries(snd[s])[r * C:r * C + C]] for s in range(N)], axis=1)
    return a[:, entries(src[r])].reshape(128, -1, 4).max(axis=2)
def reference(x, w1, w2, snd1, src1, snd2, src2):
    q = [mx_ref.quantize(x[r]) for r in range(N)]
    Z = [[mx_ref.matmul(mx_ref.quantize(cut(w1[r], i)), q[r]) for r in range(N)] for i in range(4)]
    U = []
    for r in range(N):
        h = tile([np.maximum(most(Z[i], snd1, src1, r, C1), np.float32(0)) * np.float32(0.05) for i in range(4)])
        U.append(mx_ref.matmul(mx_ref.quantize(w2[r]), mx_ref.quantize(h)))
    return {"y": np.stack([most(U, snd2, src2, r, C2) for r in range(N)])}

@@ -1,0 +1,412 @@
+from concourse.bass import DstId, RemoteDMATransfer
+from concourse.mybir import dt, AluOpType, ActivationFunctionType
+
+N = 8
+SIM_CORES = 128
+NODES, TARGETS, C1, C2 = 512, 256, 320, 64
+W = NODES + N * C1
+U = NODES + N * C2
+S1W, S2W = N * C1 // 16, N * C2 // 16
+R1W, R2W = 4 * NODES // 16, 4 * TARGETS // 16
+MXC, MXS = "float8_e4m3fn_x4", "uint8"
+
+SCRATCH = {
+    "xs": ("sbuf", [128, 4 * NODES], "bfloat16"),
+    "w1s": ("sbuf", [128, 4 * 512], "bfloat16"),
+    "w2s": ("sbuf", [128, 4 * 128], "bfloat16"),
+    "lsa": ("sbuf", [128, S1W], "int32"),
+    "lsb": ("sbuf", [128, S2W], "int32"),
+    "lra": ("sbuf", [128, R1W], "int32"),
+    "lrb": ("sbuf", [128, R2W], "int32"),
+    "osa": ("sbuf", [128, 4 * S1W], "uint16"),
+    "osb": ("sbuf", [128, 4 * S2W], "uint16"),
+    "ora": ("sbuf", [128, R1W], "uint16"),
+    "orb": ("sbuf", [128, R2W], "uint16"),
+    "xg": ("sbuf", [128, 4 * N * C1], "bfloat16"),
+    "xsc": ("sbuf", [128, N * C1], MXC), "xss": ("sbuf", [128, N * C1], MXS),
+    "xoc": ("sbuf", [128, NODES], MXC), "xos": ("sbuf", [128, NODES], MXS),
+    "xrc": ("sbuf", [128, N * C1], MXC), "xrs": ("sbuf", [128, N * C1], MXS),
+    "w1c": ("sbuf", [128, 512], MXC), "w1p": ("sbuf", [128, 512], MXS),
+    "w2c": ("sbuf", [128, 128], MXC), "w2p": ("sbuf", [128, 128], MXS),
+    "tb0": ("sbuf", [128, W], "bfloat16"), "tb1": ("sbuf", [128, W], "bfloat16"),
+    "tb2": ("sbuf", [128, W], "bfloat16"), "tb3": ("sbuf", [128, W], "bfloat16"),
+    "gg0": ("sbuf", [128, 4 * NODES], "bfloat16"), "gg1": ("sbuf", [128, 4 * NODES], "bfloat16"),
+    "gg2": ("sbuf", [128, 4 * NODES], "bfloat16"), "gg3": ("sbuf", [128, 4 * NODES], "bfloat16"),
+    "sc0": ("sbuf", [128, 4 * NODES], "bfloat16"), "sc1": ("sbuf", [128, 4 * NODES], "bfloat16"),
+    "sc2": ("sbuf", [128, 4 * NODES], "bfloat16"), "sc3": ("sbuf", [128, 4 * NODES], "bfloat16"),
+    "mk": ("sbuf", [128, 4 * NODES], "bfloat16"),
+    "ht": ("sbuf", [128, 4 * NODES], "bfloat16"),
+    "hg": ("sbuf", [128, 4 * N * C2], "bfloat16"),
+    "hsc": ("sbuf", [128, N * C2], MXC), "hss": ("sbuf", [128, N * C2], MXS),
+    "hoc": ("sbuf", [128, NODES + C2], MXC), "hos": ("sbuf", [128, NODES + C2], MXS),
+    "hrc": ("sbuf", [128, N * C2], MXC), "hrs": ("sbuf", [128, N * C2], MXS),
+    "ut": ("sbuf", [128, U], "float32"),
+    "g2": ("sbuf", [128, 4 * TARGETS], "float32"),
+    "m2": ("sbuf", [128, 2 * TARGETS], "float32"),
+    "yo": ("sbuf", [128, TARGETS], "float32"),
+    "f1c": ("sbuf", [128, 2 * C1], MXC), "f1s": ("sbuf", [128, 2 * C1], MXS),
+    "f2c": ("sbuf", [128, 2 * C2], MXC), "f2s": ("sbuf", [128, 2 * C2], MXS),
+    "pp": ("psum", [128, 512 * 8], "float32"),
+}
+SEMAPHORES = (["v", "s", "t", "loc", "dx", "dw1", "dw2", "dsa", "dsb", "dra", "drb", "dy"]
+              + ["fc1", "fs1", "fc1b", "fs1b", "fc2", "fs2"]
+              + ["x%d" % r for r in range(N)] + ["h%d" % r for r in range(N)])
+
+MATE, DIE, DIRECT, OWN = "mate", "die", "direct", "own"
+
+
+def layout(T, topo):
+    chips, ranks = [], {}
+    for r, c in enumerate(T.cores):
+        ch = topo.chip(c)
+        if ch not in ranks:
+            chips.append(ch)
+            ranks[ch] = []
+        ranks[ch].append(r)
+    roads = {}
+    for ia, a in enumerate(chips):
+        for ib, b in enumerate(chips):
+            if a == b:
+                roads[a, b] = (OWN, None)
+                continue
+            src, dst = T.cores[ranks[a][0]], T.cores[ranks[b][0]]
+            k = len(ranks[b])
+            if topo.same_plane(a, b):
+                mid = [c for c in topo.cores_of(src) if topo.die(c) != topo.die(src) and topo.may_write(c, dst)
+                       and T.rank_of(c) is None]
+                roads[a, b] = (DIE, mid[:k])
+            elif (ib - ia) % len(chips) == 1:
+                roads[a, b] = (DIRECT, None)
+            else:
+                mid = [c for c in range(SIM_CORES) if topo.mates(topo.chip(c), b) and topo.die(c) == topo.die(dst)
+                       and topo.may_write(c, dst) and topo.may_write(src, c) and T.rank_of(c) is None]
+                roads[a, b] = (MATE, mid[:k])
+    return chips, ranks, roads
+
+
+def bits(engines):
+    m = 0
+    for e in engines:
+        m |= 1 << e
+    return m
+
+
+def u8(view):
+    return view.bitcast(dt.uint8)
+
+
+HA = 128
+HB = C1 - HA
+
+
+def part(k, h):
+    return ((HB, C1), (0, HB))[h] if k == 0 else ((0, HA), (HA, C1))[h]
+
+
+HOPS = (
+    {"n": HA, "at": 0, "fc": "f1c", "fs": "f1s", "sc": "fc1", "ss": "fs1", "arr": "x", "add": 0, "C": C1, "rc": "xrc", "rs": "xrs"},
+    {"n": HB, "at": 2 * HA, "fc": "f1c", "fs": "f1s", "sc": "fc1b", "ss": "fs1b", "arr": "x", "add": 1, "C": C1, "rc": "xrc", "rs": "xrs"},
+    {"n": C2, "at": 0, "fc": "f2c", "fs": "f2s", "sc": "fc2", "ss": "fs2", "arr": "h", "add": 0, "C": C2, "rc": "hrc", "rs": "hrs"},
+)
+
+
+def hand_on(g, core, T, topo):
+    chips, ranks, roads = layout(T, topo)
+    for (a, b), (road, mid) in roads.items():
+        if not mid or core not in mid:
+            continue
+        dst = T.cores[ranks[b][mid.index(core)]]
+        rid, pid, _ = topo.addr(dst)
+        eng = topo.engines(core, dst)
+        s0, n = ranks[a][0], len(ranks[a])
+        w = len(send_engines(T.cores[s0], mid[0], T, topo)) // len(mid)
+        for H in HOPS:
+            f0, f1 = H["at"], H["at"] + n * H["n"]
+            d0 = s0 * H["C"] + f0
+            d1 = d0 + f1 - f0
+            arr = T.sem["%s%d" % (H["arr"], s0 + H["add"])]
+            g.wait_ge(T.sem[H["sc"]], n * w)
+            g.remote_dma(u8(T[H["rc"]][:, d0:d1]), u8(T[H["fc"]][:, f0:f1]), arr, T.sem.loc, pid, rid, bits(eng))
+            g.wait_ge(T.sem[H["ss"]], n * w)
+            g.remote_dma(T[H["rs"]][:, d0:d1], T[H["fs"]][:, f0:f1], arr, T.sem.loc, pid, rid, bits(eng))
+        g.wait_ge(T.sem.loc, 2 * len(HOPS) * len(eng))
+
+
+def send_engines(src, dst, T, topo):
+    e = topo.engines(src, dst)
+    if topo.chip(src) != topo.chip(dst):
+        return e
+    far = [c for c in T.cores if topo.chip(c) != topo.chip(src)][0]
+    off = topo.engines(src, far)
+    return [k for k in e if k not in off]
+
+
+def join(runs):
+    out = []
+    for a, b in sorted(runs):
+        if out and out[-1][1] == a:
+            out[-1] = (out[-1][0], b)
+        else:
+            out.append((a, b))
+    return out
+
+
+def rank_program(g, core, T, topo):
+    rank = T.rank_of(core)
+    if rank is None:
+        hand_on(g, core, T, topo)
+        return
+    chips, ranks, roads = layout(T, topo)
+    me = topo.chip(core)
+    mine = ranks[me].index(rank)
+    near = [r for r in ranks[me] if r != rank]
+    goes = {roads[me, b][0]: b for b in chips}
+    came = {roads[a, me][0]: a for a in chips}
+    v_, s_, t_ = g.vector, g.scalar, g.tensor
+    A, F = AluOpType, ActivationFunctionType
+    cnt = {"v": 0, "s": 0, "t": 0}
+    seen = {}
+    queues = {"g": g, "v": v_, "s": s_, "t": t_, "y": g.sync}
+
+    def done(ins, q):
+        ins.then_inc(T.sem[q], 1)
+        cnt[q] += 1
+        return cnt[q]
+
+    def wait(q, sem, val):
+        if val > seen.get((q, sem), 0):
+            seen[q, sem] = val
+            queues[q].wait_ge(T.sem[sem], val)
+
+    def load_list(q, buf, src, sem, ks):
+        for k in ks:
+            q.dma_start(T[buf][16 * k:16 * k + 16, :], T[src][:, :]).then_inc(T.sem[sem], 16)
+
+    load_list(g.sync, "lsa", "snd1", "dsa", range(0, 4))
+    load_list(s_, "lsa", "snd1", "dsa", range(4, 8))
+    g.sync.dma_start(T.xs[:, :], T.x[:, :]).then_inc(T.sem.dx, 16)
+    g.sync.dma_start(T.w1s[:, :], T.w1[:, :]).then_inc(T.sem.dw1, 16)
+    g.sync.dma_start(T.w2s[:, :], T.w2[:, :]).then_inc(T.sem.dw2, 16)
+    load_list(g.sync, "lra", "src1", "dra", range(8))
+    load_list(g.sync, "lsb", "snd2", "dsb", range(8))
+    load_list(g.sync, "lrb", "src2", "drb", range(8))
+
+    for t in range(4):
+        done(v_.memset(T.mk[:, t:4 * NODES:4], 1.0 if t else 0.0), "v")
+    for i in range(4):
+        done(v_.memset(T["tb%d" % i][:, NODES + rank * C1:NODES + (rank + 1) * C1], 0.0), "v")
+    const = done(v_.memset(T.ut[:, NODES + rank * C2:NODES + (rank + 1) * C2], 0.0), "v")
+
+    wait("v", "dsa", 128)
+    osa = {}
+    for t in (2, 3, 0, 1):
+        osa[t] = done(v_.tensor_scalar(T.osa[:, S1W * t:S1W * (t + 1)], T.lsa[:, :], 4, t, A.mult, A.add), "v")
+
+    def pick(q, out, win, offs, lw, t, c0, c1):
+        o = T[out][:, 4 * c0 + t:4 * c1:4]
+        i = T[win][:, 0:4 * NODES].indirect(T[offs][:, lw * t + c0 // 16:lw * t + c1 // 16])
+        return done(v_.tensor_copy(o, i), "v") if q == "v" else done(s_.activation(o, i, F.Copy), "s")
+
+    def gather(out, win, offs, lw, runs, ready, codes, planes):
+        load = {"s": 0.0, "v": sum(12 + 1.1 * (b - a) for a, b in runs)}
+        last = {"s": 0, "v": 0}
+        for a, b in runs:
+            for t in (2, 3, 0, 1):
+                for a1, b1 in [(a, b)] if b - a < 512 else [(a, a + C1), (a + C1, b)]:
+                    q = "s" if load["s"] <= load["v"] else "v"
+                    load[q] += 60 + 1.6 * (b1 - a1)
+                    wait(q, "v", ready[t])
+                    last[q] = pick(q, out, win, offs, lw, t, a1, b1)
+        wait("v", "v", last["v"])
+        wait("v", "s", last["s"])
+        for a, b in runs:
+            for k in range(a, b, 512):
+                e = min(b, k + 512)
+                qd = done(v_.quantize_mx(T[codes][:, k:e], T[planes][:, k:e], T[out][:, 4 * k:4 * e]), "v")
+        return qd
+
+    def send(items, sc, ss):
+        for m in (0, 1):
+            tr = []
+            for c, bufs, d0, sems, c0, n, eng in items:
+                d, s = T[bufs[m]][:, d0:d0 + n], T[(sc, ss)[m]][:, c0:c0 + n]
+                if m == 0:
+                    d, s = u8(d), u8(s)
+                rid, pid, _ = topo.addr(c)
+                tr.append(RemoteDMATransfer(dst_ids=[DstId(rid=rid, pnc=pid)], dma_engine_mask=bits(eng),
+                                            remote_sem=T.sem[sems[m]], src=s, dst=d))
+            g.remote_dma_fused(tr, local_sem=T.sem.loc)
+        return 2 * sum(len(x[6]) for x in items)
+
+    def share(road):
+        b = goes[road]
+        rs = [r for r in ranks[b] if r != rank]
+        to = roads[me, b][1] or [T.cores[r] for r in rs]
+        eng = send_engines(core, to[0], T, topo)
+        w = len(eng) // len(to)
+        return [(ranks[b].index(r), r, c, eng[w * k:w * k + w]) for k, (r, c) in enumerate(zip(rs, to))]
+
+    sent = 0
+    wait("v", "dx", 16)
+    wait("s", "dx", 16)
+    for h in (0, 1):
+        H = HOPS[h]
+        items = []
+        for road in (MATE, DIE):
+            for k, r, c, eng in share(road):
+                a, b = part(k, h)
+                items.append((c, (H["fc"], H["fs"]), H["at"] + mine * H["n"], (H["sc"], H["ss"]), r * C1 + a, b - a, eng))
+        qd = gather("xg", "xs", "osa", S1W, join([(x[4], x[4] + x[5]) for x in items]), osa, "xsc", "xss")
+        wait("g", "v", qd)
+        sent += send(items, "xsc", "xss")
+    for road in (DIRECT, OWN):
+        items = [(c, ("xrc", "xrs"), rank * C1, ("x%d" % rank,) * 2, r * C1, C1, eng) for k, r, c, eng in share(road)]
+        qd = gather("xg", "xs", "osa", S1W, join([(x[4], x[4] + x[5]) for x in items]), osa, "xsc", "xss")
+        wait("g", "v", qd)
+        sent += send(items, "xsc", "xss")
+
+    wait("v", "dw1", 16)
+    done(v_.quantize_mx(T.w1c[:, :], T.w1p[:, :], T.w1s[:, :]), "v")
+    qx = done(v_.quantize_mx(T.xoc[:, :], T.xos[:, :], T.xs[:, :]), "v")
+    wait("v", "dw2", 16)
+    done(v_.quantize_mx(T.w2c[:, :], T.w2p[:, :], T.w2s[:, :]), "v")
+    wait("v", "dra", 128)
+    ora = done(v_.tensor_copy(T.ora[:, :], T.lra[:, :]), "v")
+    wait("v", "dsb", 128)
+    for t in range(4):
+        osb = done(v_.tensor_scalar(T.osb[:, S2W * t:S2W * (t + 1)], T.lsb[:, :], 4, t, A.mult, A.add), "v")
+    wait("v", "drb", 128)
+    orb = done(v_.tensor_copy(T.orb[:, :], T.lrb[:, :]), "v")
+
+    def full(road):
+        a = came[road]
+        mid = roads[a, me][1]
+        if mid:
+            return 2 * len(topo.engines(mid[mine], core))
+        e = send_engines(T.cores[near[0] if road == OWN else ranks[a][0]], core, T, topo)
+        return 2 * len(e) // (1 if road == OWN else len(ranks[me]))
+
+    blocks = [("xoc", "xos", 0, NODES, [(0, NODES, 0)], None, 0)]
+
+    def two_hop(road, h):
+        H, s0, n = HOPS[h], ranks[came[road]][0], len(ranks[came[road]])
+        outs = [(k * H["n"], H["n"], NODES + (s0 + k) * C1 + part(mine, h)[0]) for k in range(n)]
+        blocks.append(("xrc", "xrs", s0 * C1 + H["at"], n * H["n"], outs, "x%d" % (s0 + h), full(road)))
+
+    def one_hop(road):
+        for r in ranks[came[road]]:
+            if r != rank:
+                blocks.append(("xrc", "xrs", r * C1, C1, [(0, C1, NODES + r * C1)], "x%d" % r, full(road)))
+
+    two_hop(DIE, 0)
+    two_hop(MATE, 0)
+    one_hop(OWN)
+    one_hop(DIRECT)
+    two_hop(DIE, 1)
+    two_hop(MATE, 1)
+    wait("t", "v", qx)
+    freed = {0: (0, 0), 1: (0, 0)}
+    for n, (cb, pb, c0, w, outs, sem, val) in enumerate(blocks):
+        if sem:
+            wait("t", sem, val)
+        half = n % 2
+        mm = []
+        for i in range(4):
+            bank = 512 * (4 * half + i)
+            wait("t", "vs"[i // 2], freed[half][i // 2])
+            mm.append(done(t_.matmul_mx(T.pp[:, bank:bank + w], T.w1c[:, 128 * i:128 * i + 128], T.w1p[:, 128 * i:128 * i + 128],
+                                        T[cb][:, c0:c0 + w], T[pb][:, c0:c0 + w], True, True), "t"))
+        for i in range(4):
+            bank = 512 * (4 * half + i)
+            q = "vs"[i // 2]
+            wait(q, "t", mm[i])
+            for z0, zn, o0 in outs:
+                out, z = T["tb%d" % i][:, o0:o0 + zn], T.pp[:, bank + z0:bank + z0 + zn]
+                if q == "v":
+                    tv = done(v_.tensor_scalar(out, z, 0.0, 0.05, A.max, A.mult), "v")
+                else:
+                    ts = done(s_.activation(out, z, F.Relu, scale=0.05), "s")
+        freed[half] = (tv, ts)
+
+    KS = 92
+    pieces = {0: [(0, KS)], 1: [(0, KS)], 2: [(0, KS)], 3: [(0, KS // 2), (KS // 2, KS)]}
+    for q in "vs":
+        wait(q, "v", max(tv, ora, const))
+        wait(q, "s", ts)
+
+    def gather1(q, i, a, b):
+        o = T["gg%d" % i][:, 16 * a:16 * b]
+        w = T["tb%d" % i][:, 0:W].indirect(T.ora[:, a:b])
+        return done(v_.tensor_copy(o, w), "v") if q == "v" else done(s_.activation(o, w, F.Copy), "s")
+
+    gs = {(i, p): gather1("s", i, p[0], p[1]) for i in range(4) for p in pieces[i]}
+    gv = {0: gather1("v", 0, KS, R1W)}
+    for i in range(4):
+        if i < 3:
+            gv[i + 1] = gather1("v", i + 1, KS, R1W)
+        for p in pieces[i]:
+            last = p is pieces[i][-1]
+            a, b = 16 * p[0], 16 * (R1W if last else p[1])
+            wait("v", "s", gs[i, p])
+            if last:
+                wait("v", "v", gv[i])
+            sc = done(v_.tensor_tensor_scan(T["sc%d" % i][:, a:b], T.mk[:, a:b], T["gg%d" % i][:, a:b], 0.0, A.mult, A.max), "v")
+            wait("v", "v", sc)
+            hd = done(v_.tensor_copy(T.ht[:, a + i:b:4], T["sc%d" % i][:, a + 3:b:4]), "v")
+
+    wait("s", "v", hd)
+    wait("v", "v", hd)
+    H = HOPS[2]
+    for pair in ((MATE, DIE), (DIRECT, OWN)):
+        items = []
+        for road in pair:
+            for k, r, c, eng in share(road):
+                if road in (MATE, DIE):
+                    items.append((c, (H["fc"], H["fs"]), H["at"] + mine * C2, (H["sc"], H["ss"]), r * C2, C2, eng))
+                elif road == DIRECT:
+                    items.append((c, ("hrc", "hrs"), rank * C2, ("h%d" % rank,) * 2, r * C2, C2, eng))
+                else:
+                    items.append((c, ("hoc", "hos"), NODES, ("h%d" % rank,) * 2, r * C2, C2, eng))
+        runs = join([(ranks[goes[road]][0] * C2, (ranks[goes[road]][-1] + 1) * C2) for road in pair])
+        qd = gather("hg", "ht", "osb", S2W, runs, {t: osb for t in range(4)}, "hsc", "hss")
+        wait("g", "v", qd)
+        sent += send(items, "hsc", "hss")
+    qh = done(v_.quantize_mx(T.hoc[:, 0:NODES], T.hos[:, 0:NODES], T.ht[:, :]), "v")
+
+    blocks = [("hoc", "hos", 0, NODES, 0, 0, []),
+              ("hoc", "hos", NODES + C2 - 128, 128, 128 - C2, NODES + near[0] * C2, [("h%d" % near[0], full(OWN))])]
+    for road in (DIRECT, DIE, MATE):
+        rs = ranks[came[road]]
+        sems = [("h%d" % r, full(road)) for r in (rs if road == DIRECT else rs[:1])]
+        blocks.append(("hrc", "hrs", rs[0] * C2, len(rs) * C2, 0, NODES + rs[0] * C2, sems))
+    wait("t", "v", qh)
+    wait("t", "s", ts)
+    uq = {"v": 0, "s": 0}
+    for n, (cb, pb, c0, w, skip, o0, sems) in enumerate(blocks):
+        for sem, val in sems:
+            wait("t", sem, val)
+        m = done(t_.matmul_mx(T.pp[:, 512 * n:512 * n + w], T.w2c[:, :], T.w2p[:, :], T[cb][:, c0:c0 + w], T[pb][:, c0:c0 + w],
+                              True, True), "t")
+        out, z = T.ut[:, o0:o0 + w - skip], T.pp[:, 512 * n + skip:512 * n + w]
+        q = "sv"[n % 2]
+        wait(q, "t", m)
+        uq[q] = done(s_.activation(out, z, F.Copy), "s") if q == "s" else done(v_.tensor_copy(out, z), "v")
+
+    wait("s", "v", max(uq["v"], orb))
+    wait("s", "s", uq["s"])
+    pcs = [(0, 16), (16, 40), (40, 64)]
+    g2 = [done(s_.activation(T.g2[:, 16 * a:16 * b], T.ut[:, 0:U].indirect(T.orb[:, a:b]), F.Copy), "s") for a, b in pcs]
+    y0 = 0
+    for (a, b), gd in zip(pcs, g2):
+        wait("v", "s", gd)
+        d = done(v_.tensor_tensor(T.m2[:, 8 * a:8 * b], T.g2[:, 16 * a:16 * b:2], T.g2[:, 16 * a + 1:16 * b:2], A.max), "v")
+        wait("v", "v", d)
+        d = done(v_.tensor_tensor(T.yo[:, 4 * a:4 * b], T.m2[:, 8 * a:8 * b:2], T.m2[:, 8 * a + 1:8 * b:2], A.max), "v")
+        if a:
+            wait("y", "v", d)
+            g.sync.dma_start(T.y[:, y0:4 * b], T.yo[:, y0:4 * b]).then_inc(T.sem.dy, 16)
+            y0 = 4 * b
+    for q in "vst":
+        wait("y", q, cnt[q])
+    g.sync.wait_ge(T.sem.dy, 32)
+    g.wait_ge(T.sem.loc, sent)

@@ -8,6 +8,7 @@ W = NODES + N * C1
 U = NODES + N * C2
 S1W, S2W = N * C1 // 16, N * C2 // 16
 R1W, R2W = 4 * NODES // 16, 4 * TARGETS // 16
+EW = NODES // 16
 MXC, MXS = "float8_e4m3fn_x4", "uint8"
 
 SCRATCH = {
@@ -19,9 +20,12 @@ SCRATCH = {
     "lra": ("sbuf", [128, R1W], "int32"),
     "lrb": ("sbuf", [128, R2W], "int32"),
     "osa": ("sbuf", [128, 4 * S1W], "uint16"),
-    "osb": ("sbuf", [128, 4 * S2W], "uint16"),
+    "osb": ("sbuf", [128, S2W], "uint16"),
     "ora": ("sbuf", [128, R1W], "uint16"),
     "orb": ("sbuf", [128, R2W], "uint16"),
+    "ecol": ("sbuf", [128, R1W], "uint16"),
+    "erow": ("dram", [16, R1W], "uint16"),
+    "ore": ("sbuf", [128, R1W], "uint16"),
     "xg": ("sbuf", [128, 4 * N * C1], "bfloat16"),
     "xsc": ("sbuf", [128, N * C1], MXC), "xss": ("sbuf", [128, N * C1], MXS),
     "xoc": ("sbuf", [128, NODES], MXC), "xos": ("sbuf", [128, NODES], MXS),
@@ -30,11 +34,12 @@ SCRATCH = {
     "w2c": ("sbuf", [128, 128], MXC), "w2p": ("sbuf", [128, 128], MXS),
     "tb0": ("sbuf", [128, W], "bfloat16"), "tb1": ("sbuf", [128, W], "bfloat16"),
     "tb2": ("sbuf", [128, W], "bfloat16"), "tb3": ("sbuf", [128, W], "bfloat16"),
-    "gg0": ("sbuf", [128, 4 * NODES], "bfloat16"), "gg1": ("sbuf", [128, 4 * NODES], "bfloat16"),
+    "gg0": ("sbuf", [128, 3 * NODES], "bfloat16"), "gg1": ("sbuf", [128, 3 * NODES], "bfloat16"),
     "gg2": ("sbuf", [128, 4 * NODES], "bfloat16"), "gg3": ("sbuf", [128, 4 * NODES], "bfloat16"),
-    "sc0": ("sbuf", [128, 4 * NODES], "bfloat16"), "sc1": ("sbuf", [128, 4 * NODES], "bfloat16"),
     "sc2": ("sbuf", [128, 4 * NODES], "bfloat16"), "sc3": ("sbuf", [128, 4 * NODES], "bfloat16"),
     "mk": ("sbuf", [128, 4 * NODES], "bfloat16"),
+    "r0": ("sbuf", [128, NODES], "bfloat16"), "r1": ("sbuf", [128, NODES], "bfloat16"),
+    "r2": ("sbuf", [128, NODES], "bfloat16"), "r3": ("sbuf", [128, NODES], "bfloat16"),
     "ht": ("sbuf", [128, 4 * NODES], "bfloat16"),
     "hg": ("sbuf", [128, 4 * N * C2], "bfloat16"),
     "hsc": ("sbuf", [128, N * C2], MXC), "hss": ("sbuf", [128, N * C2], MXS),
@@ -48,8 +53,8 @@ SCRATCH = {
     "f2c": ("sbuf", [128, 2 * C2], MXC), "f2s": ("sbuf", [128, 2 * C2], MXS),
     "pp": ("psum", [128, 512 * 8], "float32"),
 }
-SEMAPHORES = (["v", "s", "t", "loc", "dx", "dw1", "dw2", "dsa", "dsb", "dra", "drb", "dy"]
-              + ["fc1", "fs1", "fc1b", "fs1b", "fc2", "fs2"]
+SEMAPHORES = (["v", "s", "t", "loc", "dx", "dw1", "dw2", "dsa", "dsb", "dra", "drb", "der", "dre", "dy"]
+              + ["fc1a", "fs1a", "fc1b", "fs1b", "fc2", "fs2"]
               + ["x%d" % r for r in range(N)] + ["h%d" % r for r in range(N)])
 
 MATE, DIE, DIRECT, OWN = "mate", "die", "direct", "own"
@@ -70,7 +75,7 @@ def layout(T, topo):
                 roads[a, b] = (OWN, None)
                 continue
             src, dst = T.cores[ranks[a][0]], T.cores[ranks[b][0]]
-            k = len(ranks[b])
+            k = len(ranks[a])
             if topo.same_plane(a, b):
                 mid = [c for c in topo.cores_of(src) if topo.die(c) != topo.die(src) and topo.may_write(c, dst)
                        and T.rank_of(c) is None]
@@ -95,41 +100,8 @@ def u8(view):
     return view.bitcast(dt.uint8)
 
 
-HA = 128
-HB = C1 - HA
-
-
-def part(k, h):
-    return ((HB, C1), (0, HB))[h] if k == 0 else ((0, HA), (HA, C1))[h]
-
-
-HOPS = (
-    {"n": HA, "at": 0, "fc": "f1c", "fs": "f1s", "sc": "fc1", "ss": "fs1", "arr": "x", "add": 0, "C": C1, "rc": "xrc", "rs": "xrs"},
-    {"n": HB, "at": 2 * HA, "fc": "f1c", "fs": "f1s", "sc": "fc1b", "ss": "fs1b", "arr": "x", "add": 1, "C": C1, "rc": "xrc", "rs": "xrs"},
-    {"n": C2, "at": 0, "fc": "f2c", "fs": "f2s", "sc": "fc2", "ss": "fs2", "arr": "h", "add": 0, "C": C2, "rc": "hrc", "rs": "hrs"},
-)
-
-
-def hand_on(g, core, T, topo):
-    chips, ranks, roads = layout(T, topo)
-    for (a, b), (road, mid) in roads.items():
-        if not mid or core not in mid:
-            continue
-        dst = T.cores[ranks[b][mid.index(core)]]
-        rid, pid, _ = topo.addr(dst)
-        eng = topo.engines(core, dst)
-        s0, n = ranks[a][0], len(ranks[a])
-        w = len(send_engines(T.cores[s0], mid[0], T, topo)) // len(mid)
-        for H in HOPS:
-            f0, f1 = H["at"], H["at"] + n * H["n"]
-            d0 = s0 * H["C"] + f0
-            d1 = d0 + f1 - f0
-            arr = T.sem["%s%d" % (H["arr"], s0 + H["add"])]
-            g.wait_ge(T.sem[H["sc"]], n * w)
-            g.remote_dma(u8(T[H["rc"]][:, d0:d1]), u8(T[H["fc"]][:, f0:f1]), arr, T.sem.loc, pid, rid, bits(eng))
-            g.wait_ge(T.sem[H["ss"]], n * w)
-            g.remote_dma(T[H["rs"]][:, d0:d1], T[H["fs"]][:, f0:f1], arr, T.sem.loc, pid, rid, bits(eng))
-        g.wait_ge(T.sem.loc, 2 * len(HOPS) * len(eng))
+def firsts(k, n):
+    return [(k + i) % n for i in range(n)]
 
 
 def send_engines(src, dst, T, topo):
@@ -139,6 +111,44 @@ def send_engines(src, dst, T, topo):
     far = [c for c in T.cores if topo.chip(c) != topo.chip(src)][0]
     off = topo.engines(src, far)
     return [k for k in e if k not in off]
+
+
+def hand_on(g, core, T, topo):
+    chips, ranks, roads = layout(T, topo)
+    for (a, b), (road, mid) in roads.items():
+        if not mid or core not in mid:
+            continue
+        k = mid.index(core)
+        s = ranks[a][k]
+        n = len(ranks[b])
+        w = len(send_engines(T.cores[s], core, T, topo))
+        sent = 0
+        for h, d in enumerate(firsts(k, n)):
+            dst = T.cores[ranks[b][d]]
+            rid, pid, _ = topo.addr(dst)
+            eng = topo.engines(core, dst)
+            arr = T.sem["x%d" % s]
+            g.wait_ge(T.sem["fc1" + "ab"[h]], w)
+            g.remote_dma(u8(T.xrc[:, s * C1:(s + 1) * C1]), u8(T.f1c[:, d * C1:(d + 1) * C1]), arr, T.sem.loc, pid, rid, bits(eng))
+            g.wait_ge(T.sem["fs1" + "ab"[h]], w)
+            g.remote_dma(T.xrs[:, s * C1:(s + 1) * C1], T.f1s[:, d * C1:(d + 1) * C1], arr, T.sem.loc, pid, rid, bits(eng))
+            sent += 2 * len(eng)
+        for sem, out, buf in (("fc2", "hrc", "f2c"), ("fs2", "hrs", "f2s")):
+            tr = []
+            for d in range(n):
+                dst = T.cores[ranks[b][d]]
+                rid, pid, _ = topo.addr(dst)
+                eng = topo.engines(core, dst)
+                e = len(eng) // n
+                o, i = T[out][:, s * C2:(s + 1) * C2], T[buf][:, d * C2:(d + 1) * C2]
+                if out == "hrc":
+                    o, i = u8(o), u8(i)
+                tr.append(RemoteDMATransfer(dst_ids=[DstId(rid=rid, pnc=pid)], dma_engine_mask=bits(eng[e * d:e * d + e]),
+                                            remote_sem=T.sem["h%d" % s], src=i, dst=o))
+                sent += e
+            g.wait_ge(T.sem[sem], w)
+            g.remote_dma_fused(tr, local_sem=T.sem.loc)
+        g.wait_ge(T.sem.loc, sent)
 
 
 def join(runs):
@@ -182,12 +192,12 @@ def rank_program(g, core, T, topo):
         for k in ks:
             q.dma_start(T[buf][16 * k:16 * k + 16, :], T[src][:, :]).then_inc(T.sem[sem], 16)
 
-    load_list(g.sync, "lsa", "snd1", "dsa", range(0, 4))
-    load_list(s_, "lsa", "snd1", "dsa", range(4, 8))
-    g.sync.dma_start(T.xs[:, :], T.x[:, :]).then_inc(T.sem.dx, 16)
+    s_.dma_start(T.xs[:, :], T.x[:, :]).then_inc(T.sem.dx, 16)
+    load_list(g.sync, "lsa", "snd1", "dsa", range(0, 5))
+    load_list(s_, "lsa", "snd1", "dsa", range(5, 8))
+    load_list(g.sync, "lra", "src1", "dra", range(8))
     g.sync.dma_start(T.w1s[:, :], T.w1[:, :]).then_inc(T.sem.dw1, 16)
     g.sync.dma_start(T.w2s[:, :], T.w2[:, :]).then_inc(T.sem.dw2, 16)
-    load_list(g.sync, "lra", "src1", "dra", range(8))
     load_list(g.sync, "lsb", "snd2", "dsb", range(8))
     load_list(g.sync, "lrb", "src2", "drb", range(8))
 
@@ -202,28 +212,45 @@ def rank_program(g, core, T, topo):
     for t in (2, 3, 0, 1):
         osa[t] = done(v_.tensor_scalar(T.osa[:, S1W * t:S1W * (t + 1)], T.lsa[:, :], 4, t, A.mult, A.add), "v")
 
-    def pick(q, out, win, offs, lw, t, c0, c1):
+    wait("v", "dra", 128)
+    for b in range(4):
+        ec = done(v_.tensor_copy(T.ecol[0:16, EW * b:EW * (b + 1)], T.lra[0:16, b:R1W:4]), "v")
+    wait("y", "v", ec)
+    for e in range(4):
+        for b in range(4):
+            g.sync.dma_start(T.erow[4 * b:4 * b + 4, EW * e:EW * (e + 1)], T.ecol[e:16:4, EW * b:EW * (b + 1)]).then_inc(T.sem.der, 16)
+    g.sync.wait_ge(T.sem.der, 256)
+    load_list(g.sync, "ore", "erow", "dre", range(8))
+
+    def pick(q, out, layer, t, c0, c1):
         o = T[out][:, 4 * c0 + t:4 * c1:4]
-        i = T[win][:, 0:4 * NODES].indirect(T[offs][:, lw * t + c0 // 16:lw * t + c1 // 16])
+        k0, k1 = c0 // 16, c1 // 16
+        if layer == 1:
+            i = T.xs[:, 0:4 * NODES].indirect(T.osa[:, S1W * t + k0:S1W * t + k1])
+        else:
+            i = T["r%d" % t][:, 0:NODES].indirect(T.osb[:, k0:k1])
         return done(v_.tensor_copy(o, i), "v") if q == "v" else done(s_.activation(o, i, F.Copy), "s")
 
-    def gather(out, win, offs, lw, runs, ready, codes, planes):
-        load = {"s": 0.0, "v": sum(12 + 1.1 * (b - a) for a, b in runs)}
-        last = {"s": 0, "v": 0}
-        for a, b in runs:
-            for t in (2, 3, 0, 1):
-                for a1, b1 in [(a, b)] if b - a < 512 else [(a, a + C1), (a + C1, b)]:
-                    q = "s" if load["s"] <= load["v"] else "v"
-                    load[q] += 60 + 1.6 * (b1 - a1)
-                    wait(q, "v", ready[t])
-                    last[q] = pick(q, out, win, offs, lw, t, a1, b1)
-        wait("v", "v", last["v"])
-        wait("v", "s", last["s"])
+    def quantise(out, runs, codes, planes):
         for a, b in runs:
             for k in range(a, b, 512):
                 e = min(b, k + 512)
                 qd = done(v_.quantize_mx(T[codes][:, k:e], T[planes][:, k:e], T[out][:, 4 * k:4 * e]), "v")
         return qd
+
+    def gather(runs, cut):
+        load = {"s": 0.0, "v": sum(12 + 1.1 * (b - a) for a, b in runs)}
+        last = {"s": 0, "v": 0}
+        for a, b in runs:
+            for t in (2, 3, 0, 1):
+                for a1, b1 in [(k, min(b, k + cut)) for k in range(a, b, cut)]:
+                    q = "s" if load["s"] <= load["v"] else "v"
+                    load[q] += 60 + 1.6 * (b1 - a1)
+                    wait(q, "v", osa[t])
+                    last[q] = pick(q, "xg", 1, t, a1, b1)
+        wait("v", "v", last["v"])
+        wait("v", "s", last["s"])
+        return quantise("xg", runs, "xsc", "xss")
 
     def send(items, sc, ss):
         for m in (0, 1):
@@ -238,30 +265,24 @@ def rank_program(g, core, T, topo):
             g.remote_dma_fused(tr, local_sem=T.sem.loc)
         return 2 * sum(len(x[6]) for x in items)
 
-    def share(road):
+    def takes(road):
         b = goes[road]
-        rs = [r for r in ranks[b] if r != rank]
-        to = roads[me, b][1] or [T.cores[r] for r in rs]
-        eng = send_engines(core, to[0], T, topo)
-        w = len(eng) // len(to)
-        return [(ranks[b].index(r), r, c, eng[w * k:w * k + w]) for k, (r, c) in enumerate(zip(rs, to))]
+        mid = roads[me, b][1]
+        ks = [k for k in firsts(mine, len(ranks[b])) if ranks[b][k] != rank]
+        return [(k, ranks[b][k], mid[mine] if mid else T.cores[ranks[b][k]]) for k in ks]
+
+    def unit(road, h):
+        k, r, c = takes(road)[h]
+        eng = send_engines(core, c, T, topo)
+        if road in (MATE, DIE):
+            return (c, ("f1c", "f1s"), k * C1, ("fc1" + "ab"[h], "fs1" + "ab"[h]), r * C1, C1, eng)
+        return (c, ("xrc", "xrs"), rank * C1, ("x%d" % rank,) * 2, r * C1, C1, eng)
 
     sent = 0
     wait("v", "dx", 16)
     wait("s", "dx", 16)
-    for h in (0, 1):
-        H = HOPS[h]
-        items = []
-        for road in (MATE, DIE):
-            for k, r, c, eng in share(road):
-                a, b = part(k, h)
-                items.append((c, (H["fc"], H["fs"]), H["at"] + mine * H["n"], (H["sc"], H["ss"]), r * C1 + a, b - a, eng))
-        qd = gather("xg", "xs", "osa", S1W, join([(x[4], x[4] + x[5]) for x in items]), osa, "xsc", "xss")
-        wait("g", "v", qd)
-        sent += send(items, "xsc", "xss")
-    for road in (DIRECT, OWN):
-        items = [(c, ("xrc", "xrs"), rank * C1, ("x%d" % rank,) * 2, r * C1, C1, eng) for k, r, c, eng in share(road)]
-        qd = gather("xg", "xs", "osa", S1W, join([(x[4], x[4] + x[5]) for x in items]), osa, "xsc", "xss")
+    for items in ([unit(MATE, 0)], [unit(DIE, 0), unit(MATE, 1)], [unit(DIE, 1), unit(DIRECT, 0)], [unit(OWN, 0), unit(DIRECT, 1)]):
+        qd = gather(join([(x[4], x[4] + C1) for x in items]), C1 if len(items) > 1 else C1 // 2)
         wait("g", "v", qd)
         sent += send(items, "xsc", "xss")
 
@@ -270,43 +291,26 @@ def rank_program(g, core, T, topo):
     qx = done(v_.quantize_mx(T.xoc[:, :], T.xos[:, :], T.xs[:, :]), "v")
     wait("v", "dw2", 16)
     done(v_.quantize_mx(T.w2c[:, :], T.w2p[:, :], T.w2s[:, :]), "v")
-    wait("v", "dra", 128)
-    ora = done(v_.tensor_copy(T.ora[:, :], T.lra[:, :]), "v")
+    done(v_.tensor_copy(T.ora[:, :], T.lra[:, :]), "v")
     wait("v", "dsb", 128)
-    for t in range(4):
-        osb = done(v_.tensor_scalar(T.osb[:, S2W * t:S2W * (t + 1)], T.lsb[:, :], 4, t, A.mult, A.add), "v")
+    done(v_.tensor_copy(T.osb[:, :], T.lsb[:, :]), "v")
     wait("v", "drb", 128)
-    orb = done(v_.tensor_copy(T.orb[:, :], T.lrb[:, :]), "v")
+    lists = done(v_.tensor_copy(T.orb[:, :], T.lrb[:, :]), "v")
 
-    def full(road):
+    def writer(road, k):
         a = came[road]
         mid = roads[a, me][1]
-        if mid:
-            return 2 * len(topo.engines(mid[mine], core))
-        e = send_engines(T.cores[near[0] if road == OWN else ranks[a][0]], core, T, topo)
-        return 2 * len(e) // (1 if road == OWN else len(ranks[me]))
+        c = mid[k] if mid else T.cores[ranks[a][k]]
+        return len(send_engines(c, core, T, topo)) if T.rank_of(c) is not None else len(topo.engines(c, core))
 
-    blocks = [("xoc", "xos", 0, NODES, [(0, NODES, 0)], None, 0)]
-
-    def two_hop(road, h):
-        H, s0, n = HOPS[h], ranks[came[road]][0], len(ranks[came[road]])
-        outs = [(k * H["n"], H["n"], NODES + (s0 + k) * C1 + part(mine, h)[0]) for k in range(n)]
-        blocks.append(("xrc", "xrs", s0 * C1 + H["at"], n * H["n"], outs, "x%d" % (s0 + h), full(road)))
-
-    def one_hop(road):
-        for r in ranks[came[road]]:
-            if r != rank:
-                blocks.append(("xrc", "xrs", r * C1, C1, [(0, C1, NODES + r * C1)], "x%d" % r, full(road)))
-
-    two_hop(DIE, 0)
-    two_hop(MATE, 0)
-    one_hop(OWN)
-    one_hop(DIRECT)
-    two_hop(DIE, 1)
-    two_hop(MATE, 1)
+    blocks = [("xoc", "xos", 0, NODES, 0, None, 0)]
+    for road, h in ((MATE, 0), (DIE, 0), (DIRECT, 0), (OWN, 0), (MATE, 1), (DIRECT, 1), (DIE, 1)):
+        ks = [k for k in firsts(mine, len(ranks[came[road]])) if ranks[came[road]][k] != rank]
+        r = ranks[came[road]][ks[h]]
+        blocks.append(("xrc", "xrs", r * C1, C1, NODES + r * C1, "x%d" % r, 2 * writer(road, ks[h])))
     wait("t", "v", qx)
     freed = {0: (0, 0), 1: (0, 0)}
-    for n, (cb, pb, c0, w, outs, sem, val) in enumerate(blocks):
+    for n, (cb, pb, c0, w, o0, sem, val) in enumerate(blocks):
         if sem:
             wait("t", sem, val)
         half = n % 2
@@ -320,64 +324,77 @@ def rank_program(g, core, T, topo):
             bank = 512 * (4 * half + i)
             q = "vs"[i // 2]
             wait(q, "t", mm[i])
-            for z0, zn, o0 in outs:
-                out, z = T["tb%d" % i][:, o0:o0 + zn], T.pp[:, bank + z0:bank + z0 + zn]
-                if q == "v":
-                    tv = done(v_.tensor_scalar(out, z, 0.0, 0.05, A.max, A.mult), "v")
-                else:
-                    ts = done(s_.activation(out, z, F.Relu, scale=0.05), "s")
+            out, z = T["tb%d" % i][:, o0:o0 + w], T.pp[:, bank:bank + w]
+            if q == "v":
+                tv = done(v_.tensor_scalar(out, z, 0.0, 0.05, A.max, A.mult), "v")
+            else:
+                ts = done(s_.activation(out, z, F.Relu, scale=0.05), "s")
         freed[half] = (tv, ts)
 
-    KS = 92
-    pieces = {0: [(0, KS)], 1: [(0, KS)], 2: [(0, KS)], 3: [(0, KS // 2), (KS // 2, KS)]}
     for q in "vs":
-        wait(q, "v", max(tv, ora, const))
+        wait(q, "dre", 128)
+        wait(q, "v", max(tv, lists, const))
         wait(q, "s", ts)
-
-    def gather1(q, i, a, b):
-        o = T["gg%d" % i][:, 16 * a:16 * b]
-        w = T["tb%d" % i][:, 0:W].indirect(T.ora[:, a:b])
-        return done(v_.tensor_copy(o, w), "v") if q == "v" else done(s_.activation(o, w, F.Copy), "s")
-
-    gs = {(i, p): gather1("s", i, p[0], p[1]) for i in range(4) for p in pieces[i]}
-    gv = {0: gather1("v", 0, KS, R1W)}
-    for i in range(4):
-        if i < 3:
-            gv[i + 1] = gather1("v", i + 1, KS, R1W)
-        for p in pieces[i]:
-            last = p is pieces[i][-1]
-            a, b = 16 * p[0], 16 * (R1W if last else p[1])
-            wait("v", "s", gs[i, p])
-            if last:
-                wait("v", "v", gv[i])
+    acc = {}
+    for i in (0, 1):
+        acc[i] = ("s", done(s_.activation(T["gg%d" % i][:, 0:NODES], T["tb%d" % i][:, 0:W].indirect(T.ore[:, 0:EW]), F.Copy), "s"))
+    pieces = {2: [(0, R1W)], 3: [(0, R1W // 2), (R1W // 2, 3 * R1W // 4), (3 * R1W // 4, R1W)]}
+    gs = {}
+    for i in (2, 3):
+        for a, b in pieces[i]:
+            gs[i, a] = done(s_.activation(T["gg%d" % i][:, 16 * a:16 * b], T["tb%d" % i][:, 0:W].indirect(T.ora[:, a:b]), F.Copy), "s")
+    for e in (1, 2, 3):
+        for i in (0, 1):
+            wait("v", *acc[i])
+            out = T["gg%d" % i][:, NODES * e:NODES * (e + 1)] if e < 3 else T["r%d" % i][:, :]
+            acc[i] = ("v", done(v_.tensor_tensor(out, T["tb%d" % i][:, 0:W].indirect(T.ore[:, EW * e:EW * (e + 1)]),
+                                                 T["gg%d" % i][:, NODES * (e - 1):NODES * e], A.max), "v"))
+    rd = {0: acc[0][1], 1: acc[1][1]}
+    for i in (2, 3):
+        for a, b in pieces[i]:
+            wait("v", "s", gs[i, a])
+            a, b = 16 * a, 16 * b
             sc = done(v_.tensor_tensor_scan(T["sc%d" % i][:, a:b], T.mk[:, a:b], T["gg%d" % i][:, a:b], 0.0, A.mult, A.max), "v")
             wait("v", "v", sc)
-            hd = done(v_.tensor_copy(T.ht[:, a + i:b:4], T["sc%d" % i][:, a + 3:b:4]), "v")
+            rd[i] = done(v_.tensor_copy(T["r%d" % i][:, a // 4:b // 4], T["sc%d" % i][:, a + 3:b:4]), "v")
 
-    wait("s", "v", hd)
-    wait("v", "v", hd)
-    H = HOPS[2]
-    for pair in ((MATE, DIE), (DIRECT, OWN)):
+    for pair, whose in (((MATE, DIE), "sssv"), ((DIRECT, OWN), "ssvv")):
         items = []
         for road in pair:
-            for k, r, c, eng in share(road):
-                if road in (MATE, DIE):
-                    items.append((c, (H["fc"], H["fs"]), H["at"] + mine * C2, (H["sc"], H["ss"]), r * C2, C2, eng))
-                elif road == DIRECT:
-                    items.append((c, ("hrc", "hrs"), rank * C2, ("h%d" % rank,) * 2, r * C2, C2, eng))
-                else:
-                    items.append((c, ("hoc", "hos"), NODES, ("h%d" % rank,) * 2, r * C2, C2, eng))
+            to = takes(road)
+            eng = send_engines(core, to[0][2], T, topo)
+            if road in (MATE, DIE):
+                items.append((to[0][2], ("f2c", "f2s"), 0, ("fc2", "fs2"), ranks[goes[road]][0] * C2, len(to) * C2, eng))
+                continue
+            e = len(eng) // len(to)
+            for n, (k, r, c) in enumerate(to):
+                bufs, at = (("hrc", "hrs"), rank * C2) if road == DIRECT else (("hoc", "hos"), NODES)
+                items.append((c, bufs, at, ("h%d" % rank,) * 2, r * C2, C2, eng[e * n:e * n + e]))
         runs = join([(ranks[goes[road]][0] * C2, (ranks[goes[road]][-1] + 1) * C2) for road in pair])
-        qd = gather("hg", "ht", "osb", S2W, runs, {t: osb for t in range(4)}, "hsc", "hss")
+        last = {}
+        for t in range(4):
+            q = whose[t]
+            for a, b in runs:
+                wait(q, "v", rd[t])
+                last[q] = pick(q, "hg", 2, t, a, b)
+        wait("v", "v", last["v"])
+        wait("v", "s", last["s"])
+        qd = quantise("hg", runs, "hsc", "hss")
         wait("g", "v", qd)
         sent += send(items, "hsc", "hss")
+    for i in (0, 1):
+        hs = done(s_.activation(T.ht[:, i:4 * NODES:4], T["r%d" % i][:, :], F.Copy), "s")
+    for i in (2, 3):
+        hv = done(v_.tensor_copy(T.ht[:, i:4 * NODES:4], T["r%d" % i][:, :]), "v")
+    wait("v", "v", hv)
+    wait("v", "s", hs)
     qh = done(v_.quantize_mx(T.hoc[:, 0:NODES], T.hos[:, 0:NODES], T.ht[:, :]), "v")
 
     blocks = [("hoc", "hos", 0, NODES, 0, 0, []),
-              ("hoc", "hos", NODES + C2 - 128, 128, 128 - C2, NODES + near[0] * C2, [("h%d" % near[0], full(OWN))])]
+              ("hoc", "hos", NODES + C2 - 128, 128, 128 - C2, NODES + near[0] * C2, [("h%d" % near[0], 2 * writer(OWN, 1 - mine))])]
     for road in (DIRECT, DIE, MATE):
         rs = ranks[came[road]]
-        sems = [("h%d" % r, full(road)) for r in (rs if road == DIRECT else rs[:1])]
+        sems = [("h%d" % r, 2 * writer(road, k) // len(ranks[me])) for k, r in enumerate(rs)]
         blocks.append(("hrc", "hrs", rs[0] * C2, len(rs) * C2, 0, NODES + rs[0] * C2, sems))
     wait("t", "v", qh)
     wait("t", "s", ts)
@@ -392,7 +409,7 @@ def rank_program(g, core, T, topo):
         wait(q, "t", m)
         uq[q] = done(s_.activation(out, z, F.Copy), "s") if q == "s" else done(v_.tensor_copy(out, z), "v")
 
-    wait("s", "v", max(uq["v"], orb))
+    wait("s", "v", uq["v"])
     wait("s", "s", uq["s"])
     pcs = [(0, 16), (16, 40), (40, 64)]
     g2 = [done(s_.activation(T.g2[:, 16 * a:16 * b], T.ut[:, 0:U].indirect(T.orb[:, a:b]), F.Copy), "s") for a, b in pcs]

@@ -8,7 +8,8 @@ W = NODES + N * C1
 U = NODES + N * C2
 S1W, S2W = N * C1 // 16, N * C2 // 16
 R1W, R2W = 4 * NODES // 16, 4 * TARGETS // 16
-EW = NODES // 16
+E1, E2 = NODES // 16, TARGETS // 16
+EW = E1 + E2
 MXC, MXS = "float8_e4m3fn_x4", "uint8"
 
 SCRATCH = {
@@ -18,14 +19,14 @@ SCRATCH = {
     "lsa": ("sbuf", [128, S1W], "int32"),
     "lsb": ("sbuf", [128, S2W], "int32"),
     "lra": ("sbuf", [128, R1W], "int32"),
-    "lrb": ("sbuf", [128, R2W], "int32"),
+    "lrb": ("sbuf", [16, R2W], "int32"),
     "osa": ("sbuf", [128, 4 * S1W], "uint16"),
     "osb": ("sbuf", [128, S2W], "uint16"),
+    "osc": ("sbuf", [128, S2W], "uint16"),
     "ora": ("sbuf", [128, R1W], "uint16"),
-    "orb": ("sbuf", [128, R2W], "uint16"),
-    "ecol": ("sbuf", [128, R1W], "uint16"),
-    "erow": ("dram", [16, R1W], "uint16"),
-    "ore": ("sbuf", [128, R1W], "uint16"),
+    "ecol": ("sbuf", [128, 4 * EW], "uint16"),
+    "erow": ("dram", [16, 4 * EW], "uint16"),
+    "ore": ("sbuf", [128, 4 * EW], "uint16"),
     "xg": ("sbuf", [128, 4 * N * C1], "bfloat16"),
     "xsc": ("sbuf", [128, N * C1], MXC), "xss": ("sbuf", [128, N * C1], MXS),
     "xoc": ("sbuf", [128, NODES], MXC), "xos": ("sbuf", [128, NODES], MXS),
@@ -39,15 +40,13 @@ SCRATCH = {
     "sc2": ("sbuf", [128, 4 * NODES], "bfloat16"), "sc3": ("sbuf", [128, 4 * NODES], "bfloat16"),
     "mk": ("sbuf", [128, 4 * NODES], "bfloat16"),
     "r0": ("sbuf", [128, NODES], "bfloat16"), "r1": ("sbuf", [128, NODES], "bfloat16"),
-    "r2": ("sbuf", [128, NODES], "bfloat16"), "r3": ("sbuf", [128, NODES], "bfloat16"),
     "ht": ("sbuf", [128, 4 * NODES], "bfloat16"),
     "hg": ("sbuf", [128, 4 * N * C2], "bfloat16"),
     "hsc": ("sbuf", [128, N * C2], MXC), "hss": ("sbuf", [128, N * C2], MXS),
     "hoc": ("sbuf", [128, NODES + C2], MXC), "hos": ("sbuf", [128, NODES + C2], MXS),
     "hrc": ("sbuf", [128, N * C2], MXC), "hrs": ("sbuf", [128, N * C2], MXS),
     "ut": ("sbuf", [128, U], "float32"),
-    "g2": ("sbuf", [128, 4 * TARGETS], "float32"),
-    "m2": ("sbuf", [128, 2 * TARGETS], "float32"),
+    "g2": ("sbuf", [128, 3 * TARGETS], "float32"),
     "yo": ("sbuf", [128, TARGETS], "float32"),
     "f1c": ("sbuf", [128, 2 * C1], MXC), "f1s": ("sbuf", [128, 2 * C1], MXS),
     "f2c": ("sbuf", [128, 2 * C2], MXC), "f2s": ("sbuf", [128, 2 * C2], MXS),
@@ -58,6 +57,10 @@ SEMAPHORES = (["v", "s", "t", "loc", "dx", "dw1", "dw2", "dsa", "dsb", "dra", "d
               + ["x%d" % r for r in range(N)] + ["h%d" % r for r in range(N)])
 
 MATE, DIE, DIRECT, OWN = "mate", "die", "direct", "own"
+
+PLAN = (("send", MATE, 0), ("self", None, 0), ("send", DIE, 0), ("hold", OWN, 0), ("send", MATE, 1), ("send", DIE, 1),
+        ("send", DIRECT, 0), ("rows", None, 0), ("take", None, 0), ("send", DIRECT, 1), ("take", OWN, 0), ("lists", None, 0),
+        ("take", MATE, 0), ("take", DIE, 0), ("take", DIRECT, 0), ("take", MATE, 1), ("take", DIE, 1), ("take", DIRECT, 1))
 
 
 def layout(T, topo):
@@ -195,11 +198,11 @@ def rank_program(g, core, T, topo):
     s_.dma_start(T.xs[:, :], T.x[:, :]).then_inc(T.sem.dx, 16)
     load_list(g.sync, "lsa", "snd1", "dsa", range(0, 5))
     load_list(s_, "lsa", "snd1", "dsa", range(5, 8))
-    load_list(g.sync, "lra", "src1", "dra", range(8))
     g.sync.dma_start(T.w1s[:, :], T.w1[:, :]).then_inc(T.sem.dw1, 16)
+    g.sync.dma_start(T.lrb[:, :], T.src2[:, :]).then_inc(T.sem.drb, 16)
+    load_list(g.sync, "lra", "src1", "dra", range(8))
     g.sync.dma_start(T.w2s[:, :], T.w2[:, :]).then_inc(T.sem.dw2, 16)
     load_list(g.sync, "lsb", "snd2", "dsb", range(8))
-    load_list(g.sync, "lrb", "src2", "drb", range(8))
 
     for t in range(4):
         done(v_.memset(T.mk[:, t:4 * NODES:4], 1.0 if t else 0.0), "v")
@@ -212,45 +215,40 @@ def rank_program(g, core, T, topo):
     for t in (2, 3, 0, 1):
         osa[t] = done(v_.tensor_scalar(T.osa[:, S1W * t:S1W * (t + 1)], T.lsa[:, :], 4, t, A.mult, A.add), "v")
 
-    wait("v", "dra", 128)
-    for b in range(4):
-        ec = done(v_.tensor_copy(T.ecol[0:16, EW * b:EW * (b + 1)], T.lra[0:16, b:R1W:4]), "v")
-    wait("y", "v", ec)
-    for e in range(4):
-        for b in range(4):
-            g.sync.dma_start(T.erow[4 * b:4 * b + 4, EW * e:EW * (e + 1)], T.ecol[e:16:4, EW * b:EW * (b + 1)]).then_inc(T.sem.der, 16)
-    g.sync.wait_ge(T.sem.der, 256)
-    load_list(g.sync, "ore", "erow", "dre", range(8))
-
     def pick(q, out, layer, t, c0, c1):
         o = T[out][:, 4 * c0 + t:4 * c1:4]
         k0, k1 = c0 // 16, c1 // 16
         if layer == 1:
             i = T.xs[:, 0:4 * NODES].indirect(T.osa[:, S1W * t + k0:S1W * t + k1])
-        else:
+        elif t < 2:
             i = T["r%d" % t][:, 0:NODES].indirect(T.osb[:, k0:k1])
+        else:
+            i = T["sc%d" % t][:, 0:4 * NODES].indirect(T.osc[:, k0:k1])
         return done(v_.tensor_copy(o, i), "v") if q == "v" else done(s_.activation(o, i, F.Copy), "s")
 
     def quantise(out, runs, codes, planes):
         for a, b in runs:
-            for k in range(a, b, 512):
-                e = min(b, k + 512)
-                qd = done(v_.quantize_mx(T[codes][:, k:e], T[planes][:, k:e], T[out][:, 4 * k:4 * e]), "v")
+            qd = done(v_.quantize_mx(T[codes][:, a:b], T[planes][:, a:b], T[out][:, 4 * a:4 * b]), "v")
         return qd
 
-    def gather(runs, cut):
-        load = {"s": 0.0, "v": sum(12 + 1.1 * (b - a) for a, b in runs)}
+    est = {"v": 0.0, "s": 0.0}
+
+    def gather(a, b):
+        n = b - a
+        k = (4 * n + (est["v"] - est["s"]) / 1.6) / 2
+        k = min(4 * n, max(0, int(round(k / 32)) * 32))
         last = {"s": 0, "v": 0}
-        for a, b in runs:
-            for t in (2, 3, 0, 1):
-                for a1, b1 in [(k, min(b, k + cut)) for k in range(a, b, cut)]:
-                    q = "s" if load["s"] <= load["v"] else "v"
-                    load[q] += 60 + 1.6 * (b1 - a1)
+        for j, t in enumerate((2, 3, 0, 1)):
+            m = a + min(n, max(0, k - j * n))
+            for q, c0, c1 in (("s", a, m), ("v", m, b)):
+                if c1 > c0:
+                    est[q] += 60 + 1.6 * (c1 - c0)
                     wait(q, "v", osa[t])
-                    last[q] = pick(q, "xg", 1, t, a1, b1)
+                    last[q] = pick(q, "xg", 1, t, c0, c1)
         wait("v", "v", last["v"])
         wait("v", "s", last["s"])
-        return quantise("xg", runs, "xsc", "xss")
+        est["v"] = max(est.values()) + 12 + 1.1 * n
+        return quantise("xg", [(a, b)], "xsc", "xss")
 
     def send(items, sc, ss):
         for m in (0, 1):
@@ -278,66 +276,94 @@ def rank_program(g, core, T, topo):
             return (c, ("f1c", "f1s"), k * C1, ("fc1" + "ab"[h], "fs1" + "ab"[h]), r * C1, C1, eng)
         return (c, ("xrc", "xrs"), rank * C1, ("x%d" % rank,) * 2, r * C1, C1, eng)
 
-    sent = 0
-    wait("v", "dx", 16)
-    wait("s", "dx", 16)
-    for items in ([unit(MATE, 0)], [unit(DIE, 0), unit(MATE, 1)], [unit(DIE, 1), unit(DIRECT, 0)], [unit(OWN, 0), unit(DIRECT, 1)]):
-        qd = gather(join([(x[4], x[4] + C1) for x in items]), C1 if len(items) > 1 else C1 // 2)
-        wait("g", "v", qd)
-        sent += send(items, "xsc", "xss")
-
-    wait("v", "dw1", 16)
-    done(v_.quantize_mx(T.w1c[:, :], T.w1p[:, :], T.w1s[:, :]), "v")
-    qx = done(v_.quantize_mx(T.xoc[:, :], T.xos[:, :], T.xs[:, :]), "v")
-    wait("v", "dw2", 16)
-    done(v_.quantize_mx(T.w2c[:, :], T.w2p[:, :], T.w2s[:, :]), "v")
-    done(v_.tensor_copy(T.ora[:, :], T.lra[:, :]), "v")
-    wait("v", "dsb", 128)
-    done(v_.tensor_copy(T.osb[:, :], T.lsb[:, :]), "v")
-    wait("v", "drb", 128)
-    lists = done(v_.tensor_copy(T.orb[:, :], T.lrb[:, :]), "v")
-
     def writer(road, k):
         a = came[road]
         mid = roads[a, me][1]
         c = mid[k] if mid else T.cores[ranks[a][k]]
         return len(send_engines(c, core, T, topo)) if T.rank_of(c) is not None else len(topo.engines(c, core))
 
-    blocks = [("xoc", "xos", 0, NODES, 0, None, 0)]
-    for road, h in ((MATE, 0), (DIE, 0), (DIRECT, 0), (OWN, 0), (MATE, 1), (DIRECT, 1), (DIE, 1)):
-        ks = [k for k in firsts(mine, len(ranks[came[road]])) if ranks[came[road]][k] != rank]
-        r = ranks[came[road]][ks[h]]
-        blocks.append(("xrc", "xrs", r * C1, C1, NODES + r * C1, "x%d" % r, 2 * writer(road, ks[h])))
-    wait("t", "v", qx)
-    freed = {0: (0, 0), 1: (0, 0)}
-    for n, (cb, pb, c0, w, o0, sem, val) in enumerate(blocks):
-        if sem:
-            wait("t", sem, val)
-        half = n % 2
+    free = {}
+    taken = {"v": 0, "s": 0}
+    half = [0]
+
+    def multiply(road, h, own):
+        if road is None:
+            cb, pb, c0, w, o0 = "xoc", "xos", 0, NODES, 0
+            wait("t", "v", own)
+        else:
+            ks = [k for k in firsts(mine, len(ranks[came[road]])) if ranks[came[road]][k] != rank]
+            r = ranks[came[road]][ks[h]]
+            cb, pb, c0, w, o0 = "xrc", "xrs", r * C1, C1, NODES + r * C1
+            wait("t", "x%d" % r, 2 * writer(road, ks[h]))
+        banks = [512 * (half[0] + i) for i in range(4)]
+        half[0] = 4 - half[0]
         mm = []
-        for i in range(4):
-            bank = 512 * (4 * half + i)
-            wait("t", "vs"[i // 2], freed[half][i // 2])
+        for i, bank in enumerate(banks):
+            if bank in free:
+                wait("t", *free[bank])
             mm.append(done(t_.matmul_mx(T.pp[:, bank:bank + w], T.w1c[:, 128 * i:128 * i + 128], T.w1p[:, 128 * i:128 * i + 128],
                                         T[cb][:, c0:c0 + w], T[pb][:, c0:c0 + w], True, True), "t"))
-        for i in range(4):
-            bank = 512 * (4 * half + i)
-            q = "vs"[i // 2]
+        for i, bank in enumerate(banks):
+            q = "s" if est["s"] <= est["v"] else "v"
+            est[q] += 50 + 1.05 * w
             wait(q, "t", mm[i])
             out, z = T["tb%d" % i][:, o0:o0 + w], T.pp[:, bank:bank + w]
             if q == "v":
-                tv = done(v_.tensor_scalar(out, z, 0.0, 0.05, A.max, A.mult), "v")
+                taken[q] = done(v_.tensor_scalar(out, z, 0.0, 0.05, A.max, A.mult), "v")
             else:
-                ts = done(s_.activation(out, z, F.Relu, scale=0.05), "s")
-        freed[half] = (tv, ts)
+                taken[q] = done(s_.activation(out, z, F.Relu, scale=0.05), "s")
+            free[bank] = (q, taken[q])
+
+    sent = 0
+    own = lists = 0
+    held = []
+    wait("v", "dx", 16)
+    wait("s", "dx", 16)
+    for what, road, h in PLAN:
+        if what in ("send", "hold"):
+            item = unit(road, h)
+            held.append(item)
+            qd = gather(item[4], item[4] + item[5])
+            if what == "send":
+                wait("g", "v", qd)
+                sent += send(held, "xsc", "xss")
+                held = []
+        elif what == "take":
+            multiply(road, h, own)
+        elif what == "self":
+            wait("v", "dw1", 16)
+            done(v_.quantize_mx(T.w1c[:, :], T.w1p[:, :], T.w1s[:, :]), "v")
+            own = done(v_.quantize_mx(T.xoc[:, :], T.xos[:, :], T.xs[:, :]), "v")
+            est["v"] += 1150
+        elif what == "rows":
+            wait("v", "dra", 128)
+            wait("v", "drb", 16)
+            for b in range(4):
+                done(v_.tensor_copy(T.ecol[0:16, EW * b:EW * b + E1], T.lra[0:16, b:R1W:4]), "v")
+                ec = done(v_.tensor_copy(T.ecol[0:16, EW * b + E1:EW * (b + 1)], T.lrb[0:16, b:R2W:4]), "v")
+            est["v"] += 560
+            wait("y", "v", ec)
+            for e in range(4):
+                for b in range(4):
+                    g.sync.dma_start(T.erow[4 * b:4 * b + 4, EW * e:EW * (e + 1)],
+                                     T.ecol[e:16:4, EW * b:EW * (b + 1)]).then_inc(T.sem.der, 16)
+            g.sync.wait_ge(T.sem.der, 256)
+            load_list(g.sync, "ore", "erow", "dre", range(8))
+        else:
+            wait("v", "dw2", 16)
+            done(v_.quantize_mx(T.w2c[:, :], T.w2p[:, :], T.w2s[:, :]), "v")
+            done(v_.tensor_copy(T.ora[:, :], T.lra[:, :]), "v")
+            wait("v", "dsb", 128)
+            done(v_.tensor_copy(T.osb[:, :], T.lsb[:, :]), "v")
+            lists = done(v_.tensor_scalar(T.osc[:, :], T.lsb[:, :], 4, 3, A.mult, A.add), "v")
+            est["v"] += 450
 
     for q in "vs":
         wait(q, "dre", 128)
-        wait(q, "v", max(tv, lists, const))
-        wait(q, "s", ts)
-    acc = {}
-    for i in (0, 1):
-        acc[i] = ("s", done(s_.activation(T["gg%d" % i][:, 0:NODES], T["tb%d" % i][:, 0:W].indirect(T.ore[:, 0:EW]), F.Copy), "s"))
+        wait(q, "v", max(taken["v"], lists, const))
+        wait(q, "s", taken["s"])
+    first = [(T["gg%d" % i][:, 0:NODES], T["tb%d" % i][:, 0:W].indirect(T.ore[:, 0:E1])) for i in (0, 1)]
+    acc = {0: ("s", done(s_.activation(*first[0], F.Copy), "s")), 1: ("v", done(v_.tensor_copy(*first[1]), "v"))}
     pieces = {2: [(0, R1W)], 3: [(0, R1W // 2), (R1W // 2, 3 * R1W // 4), (3 * R1W // 4, R1W)]}
     gs = {}
     for i in (2, 3):
@@ -347,18 +373,16 @@ def rank_program(g, core, T, topo):
         for i in (0, 1):
             wait("v", *acc[i])
             out = T["gg%d" % i][:, NODES * e:NODES * (e + 1)] if e < 3 else T["r%d" % i][:, :]
-            acc[i] = ("v", done(v_.tensor_tensor(out, T["tb%d" % i][:, 0:W].indirect(T.ore[:, EW * e:EW * (e + 1)]),
+            acc[i] = ("v", done(v_.tensor_tensor(out, T["tb%d" % i][:, 0:W].indirect(T.ore[:, EW * e:EW * e + E1]),
                                                  T["gg%d" % i][:, NODES * (e - 1):NODES * e], A.max), "v"))
     rd = {0: acc[0][1], 1: acc[1][1]}
     for i in (2, 3):
         for a, b in pieces[i]:
             wait("v", "s", gs[i, a])
             a, b = 16 * a, 16 * b
-            sc = done(v_.tensor_tensor_scan(T["sc%d" % i][:, a:b], T.mk[:, a:b], T["gg%d" % i][:, a:b], 0.0, A.mult, A.max), "v")
-            wait("v", "v", sc)
-            rd[i] = done(v_.tensor_copy(T["r%d" % i][:, a // 4:b // 4], T["sc%d" % i][:, a + 3:b:4]), "v")
+            rd[i] = done(v_.tensor_tensor_scan(T["sc%d" % i][:, a:b], T.mk[:, a:b], T["gg%d" % i][:, a:b], 0.0, A.mult, A.max), "v")
 
-    for pair, whose in (((MATE, DIE), "sssv"), ((DIRECT, OWN), "ssvv")):
+    for pair, whose in (((MATE, DIE), ("ss", "ss", "sv", "vv")), ((DIRECT, OWN), ("ss", "ss", "vv", "vv"))):
         items = []
         for road in pair:
             to = takes(road)
@@ -370,22 +394,22 @@ def rank_program(g, core, T, topo):
             for n, (k, r, c) in enumerate(to):
                 bufs, at = (("hrc", "hrs"), rank * C2) if road == DIRECT else (("hoc", "hos"), NODES)
                 items.append((c, bufs, at, ("h%d" % rank,) * 2, r * C2, C2, eng[e * n:e * n + e]))
-        runs = join([(ranks[goes[road]][0] * C2, (ranks[goes[road]][-1] + 1) * C2) for road in pair])
+        cols = [(ranks[goes[road]][0] * C2, (ranks[goes[road]][-1] + 1) * C2) for road in pair]
         last = {}
         for t in range(4):
-            q = whose[t]
-            for a, b in runs:
-                wait(q, "v", rd[t])
-                last[q] = pick(q, "hg", 2, t, a, b)
+            for q in "sv":
+                for a, b in join([c for c, w in zip(cols, whose[t]) if w == q]):
+                    wait(q, "v", max(rd[t], lists))
+                    last[q] = pick(q, "hg", 2, t, a, b)
         wait("v", "v", last["v"])
         wait("v", "s", last["s"])
-        qd = quantise("hg", runs, "hsc", "hss")
+        qd = quantise("hg", join(cols), "hsc", "hss")
         wait("g", "v", qd)
         sent += send(items, "hsc", "hss")
     for i in (0, 1):
         hs = done(s_.activation(T.ht[:, i:4 * NODES:4], T["r%d" % i][:, :], F.Copy), "s")
     for i in (2, 3):
-        hv = done(v_.tensor_copy(T.ht[:, i:4 * NODES:4], T["r%d" % i][:, :]), "v")
+        hv = done(v_.tensor_copy(T.ht[:, i:4 * NODES:4], T["sc%d" % i][:, 3:4 * NODES:4]), "v")
     wait("v", "v", hv)
     wait("v", "s", hs)
     qh = done(v_.quantize_mx(T.hoc[:, 0:NODES], T.hos[:, 0:NODES], T.ht[:, :]), "v")
@@ -397,7 +421,7 @@ def rank_program(g, core, T, topo):
         sems = [("h%d" % r, 2 * writer(road, k) // len(ranks[me])) for k, r in enumerate(rs)]
         blocks.append(("hrc", "hrs", rs[0] * C2, len(rs) * C2, 0, NODES + rs[0] * C2, sems))
     wait("t", "v", qh)
-    wait("t", "s", ts)
+    wait("t", "s", taken["s"])
     uq = {"v": 0, "s": 0}
     for n, (cb, pb, c0, w, skip, o0, sems) in enumerate(blocks):
         for sem, val in sems:
@@ -409,20 +433,24 @@ def rank_program(g, core, T, topo):
         wait(q, "t", m)
         uq[q] = done(s_.activation(out, z, F.Copy), "s") if q == "s" else done(v_.tensor_copy(out, z), "v")
 
-    wait("s", "v", uq["v"])
-    wait("s", "s", uq["s"])
-    pcs = [(0, 16), (16, 40), (40, 64)]
-    g2 = [done(s_.activation(T.g2[:, 16 * a:16 * b], T.ut[:, 0:U].indirect(T.orb[:, a:b]), F.Copy), "s") for a, b in pcs]
-    y0 = 0
-    for (a, b), gd in zip(pcs, g2):
-        wait("v", "s", gd)
-        d = done(v_.tensor_tensor(T.m2[:, 8 * a:8 * b], T.g2[:, 16 * a:16 * b:2], T.g2[:, 16 * a + 1:16 * b:2], A.max), "v")
-        wait("v", "v", d)
-        d = done(v_.tensor_tensor(T.yo[:, 4 * a:4 * b], T.m2[:, 8 * a:8 * b:2], T.m2[:, 8 * a + 1:8 * b:2], A.max), "v")
-        if a:
-            wait("y", "v", d)
-            g.sync.dma_start(T.y[:, y0:4 * b], T.yo[:, y0:4 * b]).then_inc(T.sem.dy, 16)
-            y0 = 4 * b
+    for q in "sv":
+        wait(q, "v", uq["v"])
+        wait(q, "s", uq["s"])
+
+    def source(e, k):
+        return T.ut[:, 0:U].indirect(T.ore[:, EW * e + E1 + E2 // 2 * k:EW * e + E1 + E2 // 2 * (k + 1)])
+
+    hw = TARGETS // 2
+    up = [("s", done(s_.activation(T.g2[:, hw * k:hw * (k + 1)], source(0, k), F.Copy), "s")) for k in (0, 1)]
+    for e in (1, 2, 3):
+        for k in (0, 1):
+            wait("v", *up[k])
+            out = T.g2[:, TARGETS * e + hw * k:TARGETS * e + hw * (k + 1)] if e < 3 else T.yo[:, hw * k:hw * (k + 1)]
+            up[k] = ("v", done(v_.tensor_tensor(out, source(e, k), T.g2[:, TARGETS * (e - 1) + hw * k:TARGETS * (e - 1) + hw * (k + 1)],
+                                                A.max), "v"))
+    for k in (0, 1):
+        wait("y", *up[k])
+        g.sync.dma_start(T.y[:, hw * k:hw * (k + 1)], T.yo[:, hw * k:hw * (k + 1)]).then_inc(T.sem.dy, 16)
     for q in "vst":
         wait("y", q, cnt[q])
     g.sync.wait_ge(T.sem.dy, 32)

from concourse.bass import DstId, RemoteDMATransfer
from concourse.mybir import dt, AluOpType, ActivationFunctionType

N = 8
SIM_CORES = 128
NODES, TARGETS, C1, C2 = 512, 256, 320, 64
W = NODES + N * C1
U = NODES + N * C2
S1W, S2W = N * C1 // 16, N * C2 // 16
R1W, R2W = 4 * NODES // 16, 4 * TARGETS // 16
E1, E2 = NODES // 16, TARGETS // 16
EW = E1 + E2
MXC, MXS = "float8_e4m3fn_x4", "uint8"

SCRATCH = {
    "xs": ("sbuf", [128, 4 * NODES], "bfloat16"),
    "w1s": ("sbuf", [128, 4 * 512], "bfloat16"),
    "w2s": ("sbuf", [128, 4 * 128], "bfloat16"),
    "lsa": ("sbuf", [128, S1W], "int32"),
    "lsb": ("sbuf", [128, S2W], "int32"),
    "lra": ("sbuf", [128, R1W], "int32"),
    "lrb": ("sbuf", [16, R2W], "int32"),
    "osa": ("sbuf", [128, 4 * S1W], "uint16"),
    "osb": ("sbuf", [128, S2W], "uint16"),
    "osc": ("sbuf", [128, S2W], "uint16"),
    "ora": ("sbuf", [128, R1W], "uint16"),
    "ecol": ("sbuf", [128, 4 * EW], "uint16"),
    "erow": ("dram", [16, 4 * EW], "uint16"),
    "ore": ("sbuf", [128, 4 * EW], "uint16"),
    "xg": ("sbuf", [128, 4 * N * C1], "bfloat16"),
    "xsc": ("sbuf", [128, N * C1], MXC), "xss": ("sbuf", [128, N * C1], MXS),
    "xoc": ("sbuf", [128, NODES], MXC), "xos": ("sbuf", [128, NODES], MXS),
    "xrc": ("sbuf", [128, N * C1], MXC), "xrs": ("sbuf", [128, N * C1], MXS),
    "w1c": ("sbuf", [128, 512], MXC), "w1p": ("sbuf", [128, 512], MXS),
    "w2c": ("sbuf", [128, 128], MXC), "w2p": ("sbuf", [128, 128], MXS),
    "tb0": ("sbuf", [128, W], "bfloat16"), "tb1": ("sbuf", [128, W], "bfloat16"),
    "tb2": ("sbuf", [128, W], "bfloat16"), "tb3": ("sbuf", [128, W], "bfloat16"),
    "gg0": ("sbuf", [128, 3 * NODES], "bfloat16"), "gg1": ("sbuf", [128, 3 * NODES], "bfloat16"),
    "gg2": ("sbuf", [128, 4 * NODES], "bfloat16"), "gg3": ("sbuf", [128, 4 * NODES], "bfloat16"),
    "sc2": ("sbuf", [128, 4 * NODES], "bfloat16"), "sc3": ("sbuf", [128, 4 * NODES], "bfloat16"),
    "mk": ("sbuf", [128, 4 * NODES], "bfloat16"),
    "r0": ("sbuf", [128, NODES], "bfloat16"), "r1": ("sbuf", [128, NODES], "bfloat16"),
    "ht": ("sbuf", [128, 4 * NODES], "bfloat16"),
    "hg": ("sbuf", [128, 4 * N * C2], "bfloat16"),
    "hsc": ("sbuf", [128, N * C2], MXC), "hss": ("sbuf", [128, N * C2], MXS),
    "hoc": ("sbuf", [128, NODES + C2], MXC), "hos": ("sbuf", [128, NODES + C2], MXS),
    "hrc": ("sbuf", [128, N * C2], MXC), "hrs": ("sbuf", [128, N * C2], MXS),
    "ut": ("sbuf", [128, U], "float32"),
    "g2": ("sbuf", [128, 3 * TARGETS], "float32"),
    "yo": ("sbuf", [128, TARGETS], "float32"),
    "f1c": ("sbuf", [128, 2 * C1], MXC), "f1s": ("sbuf", [128, 2 * C1], MXS),
    "f2c": ("sbuf", [128, 2 * C2], MXC), "f2s": ("sbuf", [128, 2 * C2], MXS),
    "pp": ("psum", [128, 512 * 8], "float32"),
}
SEMAPHORES = (["v", "s", "t", "loc", "dx", "dw1", "dw2", "dsa", "dsb", "dra", "drb", "der", "dre", "dy"]
              + ["fc1a", "fs1a", "fc1b", "fs1b", "fc2", "fs2"]
              + ["x%d" % r for r in range(N)] + ["h%d" % r for r in range(N)])

MATE, DIE, DIRECT, OWN = "mate", "die", "direct", "own"

PLAN = (("send", MATE, 0), ("self", None, 0), ("send", DIE, 0), ("hold", OWN, 0), ("send", MATE, 1), ("send", DIE, 1),
        ("send", DIRECT, 0), ("rows", None, 0), ("take", None, 0), ("send", DIRECT, 1), ("take", OWN, 0), ("lists", None, 0),
        ("take", MATE, 0), ("take", DIE, 0), ("take", DIRECT, 0), ("take", MATE, 1), ("take", DIE, 1), ("take", DIRECT, 1))


def layout(T, topo):
    chips, ranks = [], {}
    for r, c in enumerate(T.cores):
        ch = topo.chip(c)
        if ch not in ranks:
            chips.append(ch)
            ranks[ch] = []
        ranks[ch].append(r)
    roads = {}
    for ia, a in enumerate(chips):
        for ib, b in enumerate(chips):
            if a == b:
                roads[a, b] = (OWN, None)
                continue
            src, dst = T.cores[ranks[a][0]], T.cores[ranks[b][0]]
            k = len(ranks[a])
            if topo.same_plane(a, b):
                mid = [c for c in topo.cores_of(src) if topo.die(c) != topo.die(src) and topo.may_write(c, dst)
                       and T.rank_of(c) is None]
                roads[a, b] = (DIE, mid[:k])
            elif (ib - ia) % len(chips) == 1:
                roads[a, b] = (DIRECT, None)
            else:
                mid = [c for c in range(SIM_CORES) if topo.mates(topo.chip(c), b) and topo.die(c) == topo.die(dst)
                       and topo.may_write(c, dst) and topo.may_write(src, c) and T.rank_of(c) is None]
                roads[a, b] = (MATE, mid[:k])
    return chips, ranks, roads


def bits(engines):
    m = 0
    for e in engines:
        m |= 1 << e
    return m


def u8(view):
    return view.bitcast(dt.uint8)


def firsts(k, n):
    return [(k + i) % n for i in range(n)]


def send_engines(src, dst, T, topo):
    e = topo.engines(src, dst)
    if topo.chip(src) != topo.chip(dst):
        return e
    far = [c for c in T.cores if topo.chip(c) != topo.chip(src)][0]
    off = topo.engines(src, far)
    return [k for k in e if k not in off]


def hand_on(g, core, T, topo):
    chips, ranks, roads = layout(T, topo)
    for (a, b), (road, mid) in roads.items():
        if not mid or core not in mid:
            continue
        k = mid.index(core)
        s = ranks[a][k]
        n = len(ranks[b])
        w = len(send_engines(T.cores[s], core, T, topo))
        sent = 0
        for h, d in enumerate(firsts(k, n)):
            dst = T.cores[ranks[b][d]]
            rid, pid, _ = topo.addr(dst)
            eng = topo.engines(core, dst)
            arr = T.sem["x%d" % s]
            g.wait_ge(T.sem["fc1" + "ab"[h]], w)
            g.remote_dma(u8(T.xrc[:, s * C1:(s + 1) * C1]), u8(T.f1c[:, d * C1:(d + 1) * C1]), arr, T.sem.loc, pid, rid, bits(eng))
            g.wait_ge(T.sem["fs1" + "ab"[h]], w)
            g.remote_dma(T.xrs[:, s * C1:(s + 1) * C1], T.f1s[:, d * C1:(d + 1) * C1], arr, T.sem.loc, pid, rid, bits(eng))
            sent += 2 * len(eng)
        for sem, out, buf in (("fc2", "hrc", "f2c"), ("fs2", "hrs", "f2s")):
            tr = []
            for d in range(n):
                dst = T.cores[ranks[b][d]]
                rid, pid, _ = topo.addr(dst)
                eng = topo.engines(core, dst)
                e = len(eng) // n
                o, i = T[out][:, s * C2:(s + 1) * C2], T[buf][:, d * C2:(d + 1) * C2]
                if out == "hrc":
                    o, i = u8(o), u8(i)
                tr.append(RemoteDMATransfer(dst_ids=[DstId(rid=rid, pnc=pid)], dma_engine_mask=bits(eng[e * d:e * d + e]),
                                            remote_sem=T.sem["h%d" % s], src=i, dst=o))
                sent += e
            g.wait_ge(T.sem[sem], w)
            g.remote_dma_fused(tr, local_sem=T.sem.loc)
        g.wait_ge(T.sem.loc, sent)


def join(runs):
    out = []
    for a, b in sorted(runs):
        if out and out[-1][1] == a:
            out[-1] = (out[-1][0], b)
        else:
            out.append((a, b))
    return out


def rank_program(g, core, T, topo):
    rank = T.rank_of(core)
    if rank is None:
        hand_on(g, core, T, topo)
        return
    chips, ranks, roads = layout(T, topo)
    me = topo.chip(core)
    mine = ranks[me].index(rank)
    near = [r for r in ranks[me] if r != rank]
    goes = {roads[me, b][0]: b for b in chips}
    came = {roads[a, me][0]: a for a in chips}
    v_, s_, t_ = g.vector, g.scalar, g.tensor
    A, F = AluOpType, ActivationFunctionType
    cnt = {"v": 0, "s": 0, "t": 0}
    seen = {}
    queues = {"g": g, "v": v_, "s": s_, "t": t_, "y": g.sync}

    def done(ins, q):
        ins.then_inc(T.sem[q], 1)
        cnt[q] += 1
        return cnt[q]

    def wait(q, sem, val):
        if val > seen.get((q, sem), 0):
            seen[q, sem] = val
            queues[q].wait_ge(T.sem[sem], val)

    def load_list(q, buf, src, sem, ks):
        for k in ks:
            q.dma_start(T[buf][16 * k:16 * k + 16, :], T[src][:, :]).then_inc(T.sem[sem], 16)

    s_.dma_start(T.xs[:, :], T.x[:, :]).then_inc(T.sem.dx, 16)
    load_list(g.sync, "lsa", "snd1", "dsa", range(0, 5))
    load_list(s_, "lsa", "snd1", "dsa", range(5, 8))
    g.sync.dma_start(T.w1s[:, :], T.w1[:, :]).then_inc(T.sem.dw1, 16)
    g.sync.dma_start(T.lrb[:, :], T.src2[:, :]).then_inc(T.sem.drb, 16)
    load_list(g.sync, "lra", "src1", "dra", range(8))
    g.sync.dma_start(T.w2s[:, :], T.w2[:, :]).then_inc(T.sem.dw2, 16)
    load_list(g.sync, "lsb", "snd2", "dsb", range(8))

    for t in range(4):
        done(v_.memset(T.mk[:, t:4 * NODES:4], 1.0 if t else 0.0), "v")
    for i in range(4):
        done(v_.memset(T["tb%d" % i][:, NODES + rank * C1:NODES + (rank + 1) * C1], 0.0), "v")
    const = done(v_.memset(T.ut[:, NODES + rank * C2:NODES + (rank + 1) * C2], 0.0), "v")

    wait("v", "dsa", 128)
    osa = {}
    for t in (2, 3, 0, 1):
        osa[t] = done(v_.tensor_scalar(T.osa[:, S1W * t:S1W * (t + 1)], T.lsa[:, :], 4, t, A.mult, A.add), "v")

    def pick(q, out, layer, t, c0, c1):
        o = T[out][:, 4 * c0 + t:4 * c1:4]
        k0, k1 = c0 // 16, c1 // 16
        if layer == 1:
            i = T.xs[:, 0:4 * NODES].indirect(T.osa[:, S1W * t + k0:S1W * t + k1])
        elif t < 2:
            i = T["r%d" % t][:, 0:NODES].indirect(T.osb[:, k0:k1])
        else:
            i = T["sc%d" % t][:, 0:4 * NODES].indirect(T.osc[:, k0:k1])
        return done(v_.tensor_copy(o, i), "v") if q == "v" else done(s_.activation(o, i, F.Copy), "s")

    def quantise(out, runs, codes, planes):
        for a, b in runs:
            qd = done(v_.quantize_mx(T[codes][:, a:b], T[planes][:, a:b], T[out][:, 4 * a:4 * b]), "v")
        return qd

    est = {"v": 0.0, "s": 0.0}

    def gather(a, b):
        n = b - a
        k = (4 * n + (est["v"] - est["s"]) / 1.6) / 2
        k = min(4 * n, max(0, int(round(k / 32)) * 32))
        last = {"s": 0, "v": 0}
        for j, t in enumerate((2, 3, 0, 1)):
            m = a + min(n, max(0, k - j * n))
            for q, c0, c1 in (("s", a, m), ("v", m, b)):
                if c1 > c0:
                    est[q] += 60 + 1.6 * (c1 - c0)
                    wait(q, "v", osa[t])
                    last[q] = pick(q, "xg", 1, t, c0, c1)
        wait("v", "v", last["v"])
        wait("v", "s", last["s"])
        est["v"] = max(est.values()) + 12 + 1.1 * n
        return quantise("xg", [(a, b)], "xsc", "xss")

    def send(items, sc, ss):
        for m in (0, 1):
            tr = []
            for c, bufs, d0, sems, c0, n, eng in items:
                d, s = T[bufs[m]][:, d0:d0 + n], T[(sc, ss)[m]][:, c0:c0 + n]
                if m == 0:
                    d, s = u8(d), u8(s)
                rid, pid, _ = topo.addr(c)
                tr.append(RemoteDMATransfer(dst_ids=[DstId(rid=rid, pnc=pid)], dma_engine_mask=bits(eng),
                                            remote_sem=T.sem[sems[m]], src=s, dst=d))
            g.remote_dma_fused(tr, local_sem=T.sem.loc)
        return 2 * sum(len(x[6]) for x in items)

    def takes(road):
        b = goes[road]
        mid = roads[me, b][1]
        ks = [k for k in firsts(mine, len(ranks[b])) if ranks[b][k] != rank]
        return [(k, ranks[b][k], mid[mine] if mid else T.cores[ranks[b][k]]) for k in ks]

    def unit(road, h):
        k, r, c = takes(road)[h]
        eng = send_engines(core, c, T, topo)
        if road in (MATE, DIE):
            return (c, ("f1c", "f1s"), k * C1, ("fc1" + "ab"[h], "fs1" + "ab"[h]), r * C1, C1, eng)
        return (c, ("xrc", "xrs"), rank * C1, ("x%d" % rank,) * 2, r * C1, C1, eng)

    def writer(road, k):
        a = came[road]
        mid = roads[a, me][1]
        c = mid[k] if mid else T.cores[ranks[a][k]]
        return len(send_engines(c, core, T, topo)) if T.rank_of(c) is not None else len(topo.engines(c, core))

    free = {}
    taken = {"v": 0, "s": 0}
    half = [0]

    def multiply(road, h, own):
        if road is None:
            cb, pb, c0, w, o0 = "xoc", "xos", 0, NODES, 0
            wait("t", "v", own)
        else:
            ks = [k for k in firsts(mine, len(ranks[came[road]])) if ranks[came[road]][k] != rank]
            r = ranks[came[road]][ks[h]]
            cb, pb, c0, w, o0 = "xrc", "xrs", r * C1, C1, NODES + r * C1
            wait("t", "x%d" % r, 2 * writer(road, ks[h]))
        banks = [512 * (half[0] + i) for i in range(4)]
        half[0] = 4 - half[0]
        mm = []
        for i, bank in enumerate(banks):
            if bank in free:
                wait("t", *free[bank])
            mm.append(done(t_.matmul_mx(T.pp[:, bank:bank + w], T.w1c[:, 128 * i:128 * i + 128], T.w1p[:, 128 * i:128 * i + 128],
                                        T[cb][:, c0:c0 + w], T[pb][:, c0:c0 + w], True, True), "t"))
        for i, bank in enumerate(banks):
            q = "s" if est["s"] <= est["v"] else "v"
            est[q] += 50 + 1.05 * w
            wait(q, "t", mm[i])
            out, z = T["tb%d" % i][:, o0:o0 + w], T.pp[:, bank:bank + w]
            if q == "v":
                taken[q] = done(v_.tensor_scalar(out, z, 0.0, 0.05, A.max, A.mult), "v")
            else:
                taken[q] = done(s_.activation(out, z, F.Relu, scale=0.05), "s")
            free[bank] = (q, taken[q])

    sent = 0
    own = lists = 0
    held = []
    wait("v", "dx", 16)
    wait("s", "dx", 16)
    for what, road, h in PLAN:
        if what in ("send", "hold"):
            item = unit(road, h)
            held.append(item)
            qd = gather(item[4], item[4] + item[5])
            if what == "send":
                wait("g", "v", qd)
                sent += send(held, "xsc", "xss")
                held = []
        elif what == "take":
            multiply(road, h, own)
        elif what == "self":
            wait("v", "dw1", 16)
            done(v_.quantize_mx(T.w1c[:, :], T.w1p[:, :], T.w1s[:, :]), "v")
            own = done(v_.quantize_mx(T.xoc[:, :], T.xos[:, :], T.xs[:, :]), "v")
            est["v"] += 1150
        elif what == "rows":
            wait("v", "dra", 128)
            wait("v", "drb", 16)
            for b in range(4):
                done(v_.tensor_copy(T.ecol[0:16, EW * b:EW * b + E1], T.lra[0:16, b:R1W:4]), "v")
                ec = done(v_.tensor_copy(T.ecol[0:16, EW * b + E1:EW * (b + 1)], T.lrb[0:16, b:R2W:4]), "v")
            est["v"] += 560
            wait("y", "v", ec)
            for e in range(4):
                for b in range(4):
                    g.sync.dma_start(T.erow[4 * b:4 * b + 4, EW * e:EW * (e + 1)],
                                     T.ecol[e:16:4, EW * b:EW * (b + 1)]).then_inc(T.sem.der, 16)
            g.sync.wait_ge(T.sem.der, 256)
            load_list(g.sync, "ore", "erow", "dre", range(8))
        else:
            wait("v", "dw2", 16)
            done(v_.quantize_mx(T.w2c[:, :], T.w2p[:, :], T.w2s[:, :]), "v")
            done(v_.tensor_copy(T.ora[:, :], T.lra[:, :]), "v")
            wait("v", "dsb", 128)
            done(v_.tensor_copy(T.osb[:, :], T.lsb[:, :]), "v")
            lists = done(v_.tensor_scalar(T.osc[:, :], T.lsb[:, :], 4, 3, A.mult, A.add), "v")
            est["v"] += 450

    for q in "vs":
        wait(q, "dre", 128)
        wait(q, "v", max(taken["v"], lists, const))
        wait(q, "s", taken["s"])
    first = [(T["gg%d" % i][:, 0:NODES], T["tb%d" % i][:, 0:W].indirect(T.ore[:, 0:E1])) for i in (0, 1)]
    acc = {0: ("s", done(s_.activation(*first[0], F.Copy), "s")), 1: ("v", done(v_.tensor_copy(*first[1]), "v"))}
    pieces = {2: [(0, R1W)], 3: [(0, R1W // 2), (R1W // 2, 3 * R1W // 4), (3 * R1W // 4, R1W)]}
    gs = {}
    for i in (2, 3):
        for a, b in pieces[i]:
            gs[i, a] = done(s_.activation(T["gg%d" % i][:, 16 * a:16 * b], T["tb%d" % i][:, 0:W].indirect(T.ora[:, a:b]), F.Copy), "s")
    for e in (1, 2, 3):
        for i in (0, 1):
            wait("v", *acc[i])
            out = T["gg%d" % i][:, NODES * e:NODES * (e + 1)] if e < 3 else T["r%d" % i][:, :]
            acc[i] = ("v", done(v_.tensor_tensor(out, T["tb%d" % i][:, 0:W].indirect(T.ore[:, EW * e:EW * e + E1]),
                                                 T["gg%d" % i][:, NODES * (e - 1):NODES * e], A.max), "v"))
    rd = {0: acc[0][1], 1: acc[1][1]}
    for i in (2, 3):
        for a, b in pieces[i]:
            wait("v", "s", gs[i, a])
            a, b = 16 * a, 16 * b
            rd[i] = done(v_.tensor_tensor_scan(T["sc%d" % i][:, a:b], T.mk[:, a:b], T["gg%d" % i][:, a:b], 0.0, A.mult, A.max), "v")

    for pair, whose in (((MATE, DIE), ("ss", "ss", "sv", "vv")), ((DIRECT, OWN), ("ss", "ss", "vv", "vv"))):
        items = []
        for road in pair:
            to = takes(road)
            eng = send_engines(core, to[0][2], T, topo)
            if road in (MATE, DIE):
                items.append((to[0][2], ("f2c", "f2s"), 0, ("fc2", "fs2"), ranks[goes[road]][0] * C2, len(to) * C2, eng))
                continue
            e = len(eng) // len(to)
            for n, (k, r, c) in enumerate(to):
                bufs, at = (("hrc", "hrs"), rank * C2) if road == DIRECT else (("hoc", "hos"), NODES)
                items.append((c, bufs, at, ("h%d" % rank,) * 2, r * C2, C2, eng[e * n:e * n + e]))
        cols = [(ranks[goes[road]][0] * C2, (ranks[goes[road]][-1] + 1) * C2) for road in pair]
        last = {}
        for t in range(4):
            for q in "sv":
                for a, b in join([c for c, w in zip(cols, whose[t]) if w == q]):
                    wait(q, "v", max(rd[t], lists))
                    last[q] = pick(q, "hg", 2, t, a, b)
        wait("v", "v", last["v"])
        wait("v", "s", last["s"])
        qd = quantise("hg", join(cols), "hsc", "hss")
        wait("g", "v", qd)
        sent += send(items, "hsc", "hss")
    for i in (0, 1):
        hs = done(s_.activation(T.ht[:, i:4 * NODES:4], T["r%d" % i][:, :], F.Copy), "s")
    for i in (2, 3):
        hv = done(v_.tensor_copy(T.ht[:, i:4 * NODES:4], T["sc%d" % i][:, 3:4 * NODES:4]), "v")
    wait("v", "v", hv)
    wait("v", "s", hs)
    qh = done(v_.quantize_mx(T.hoc[:, 0:NODES], T.hos[:, 0:NODES], T.ht[:, :]), "v")

    blocks = [("hoc", "hos", 0, NODES, 0, 0, []),
              ("hoc", "hos", NODES + C2 - 128, 128, 128 - C2, NODES + near[0] * C2, [("h%d" % near[0], 2 * writer(OWN, 1 - mine))])]
    for road in (DIRECT, DIE, MATE):
        rs = ranks[came[road]]
        sems = [("h%d" % r, 2 * writer(road, k) // len(ranks[me])) for k, r in enumerate(rs)]
        blocks.append(("hrc", "hrs", rs[0] * C2, len(rs) * C2, 0, NODES + rs[0] * C2, sems))
    wait("t", "v", qh)
    wait("t", "s", taken["s"])
    uq = {"v": 0, "s": 0}
    for n, (cb, pb, c0, w, skip, o0, sems) in enumerate(blocks):
        for sem, val in sems:
            wait("t", sem, val)
        m = done(t_.matmul_mx(T.pp[:, 512 * n:512 * n + w], T.w2c[:, :], T.w2p[:, :], T[cb][:, c0:c0 + w], T[pb][:, c0:c0 + w],
                              True, True), "t")
        out, z = T.ut[:, o0:o0 + w - skip], T.pp[:, 512 * n + skip:512 * n + w]
        q = "sv"[n % 2]
        wait(q, "t", m)
        uq[q] = done(s_.activation(out, z, F.Copy), "s") if q == "s" else done(v_.tensor_copy(out, z), "v")

    for q in "sv":
        wait(q, "v", uq["v"])
        wait(q, "s", uq["s"])

    def source(e, k):
        return T.ut[:, 0:U].indirect(T.ore[:, EW * e + E1 + E2 // 2 * k:EW * e + E1 + E2 // 2 * (k + 1)])

    hw = TARGETS // 2
    up = [("s", done(s_.activation(T.g2[:, hw * k:hw * (k + 1)], source(0, k), F.Copy), "s")) for k in (0, 1)]
    for e in (1, 2, 3):
        for k in (0, 1):
            wait("v", *up[k])
            out = T.g2[:, TARGETS * e + hw * k:TARGETS * e + hw * (k + 1)] if e < 3 else T.yo[:, hw * k:hw * (k + 1)]
            up[k] = ("v", done(v_.tensor_tensor(out, source(e, k), T.g2[:, TARGETS * (e - 1) + hw * k:TARGETS * (e - 1) + hw * (k + 1)],
                                                A.max), "v"))
    for k in (0, 1):
        wait("y", *up[k])
        g.sync.dma_start(T.y[:, hw * k:hw * (k + 1)], T.yo[:, hw * k:hw * (k + 1)]).then_inc(T.sem.dy, 16)
    for q in "vst":
        wait("y", q, cnt[q])
    g.sync.wait_ge(T.sem.dy, 32)
    g.wait_ge(T.sem.loc, sent)
